import numpy as np
import ml_dtypes


def mxq(x, axis, fmt="e4m3"):
    dtype, down = {"e4m3": (ml_dtypes.float8_e4m3fn, 7), "e5m2": (ml_dtypes.float8_e5m2, 14)}[fmt]
    v = np.moveaxis(np.asarray(x, np.float32).astype(ml_dtypes.bfloat16).astype(np.float64), axis, -1)
    blocks = v.reshape(v.shape[:-1] + (-1, 32))
    amax = np.abs(blocks).max(-1, keepdims=True)
    byte = np.maximum(np.where(amax > 0, np.frexp(amax)[1] - 1 + 127, 0) - down, 1)
    scale = np.exp2(byte - 127.0)
    codes = (blocks / scale).astype(np.float32).astype(dtype).astype(np.float64)
    return np.moveaxis((codes * scale).reshape(v.shape), -1, axis)


WIDE = False


def mx_kscale(k):
    if not WIDE:
        return np.ones(k)
    levels = np.array([10, -10, 5, -5, 0])
    if k % 512:
        return np.exp2(np.random.permutation(np.resize(levels, k // 32))).repeat(32)
    a = np.empty((k // 512, 16))
    for p in range(k // 512):
        a[p, :8] = np.random.permutation(np.resize(levels, 8))
        for g in range(8):
            far = levels[np.abs(levels - a[p, g]) >= 10]
            a[p, g + 8] = far[np.random.randint(len(far))]
    return np.exp2(a.ravel()).repeat(32)


def f64(x):
    return np.asarray(x).astype(np.float64)


def striped(idx):
    return np.tile(idx.reshape(-1, 16).T, (8, 1)).astype(np.uint16)


def unstriped(offs):
    return offs[:16].T.reshape(-1).astype(np.int64)


def pack_weight(w):
    k, n = w.shape
    w = f64(np.asarray(w, np.float32).astype(ml_dtypes.bfloat16)).reshape(k // 32, 32, n)
    amax = np.abs(w).max(1)
    byte = np.clip(np.where(amax > 0, np.frexp(amax)[1] - 1 + 127 - 7, 1), 1, 254)
    scaled = (w * np.exp2(127.0 - byte)[:, None, :]).reshape(k, n).astype(np.float32)
    words = np.ascontiguousarray(scaled.reshape(k // 512, 128, 4, n).transpose(0, 1, 3, 2)).astype(ml_dtypes.float8_e4m3fn).view(np.uint8)
    return words, np.ascontiguousarray(byte.astype(np.uint8).reshape(k // 512, 16, n))


def unpack_weight(words, scales):
    g, p, n, _ = words.shape
    vals = np.ascontiguousarray(words).view(ml_dtypes.float8_e4m3fn).astype(np.float64) * np.repeat(np.exp2(scales.astype(np.float64) - 127.0), 8, axis=1)[..., None]
    return vals.transpose(0, 1, 3, 2).reshape(g * 512, n)


def relu(v):
    return np.maximum(v, 0.0)


K, T, E, C, N = 1024, 512, 4, 128, 128


def by_expert(wq, xq):
    return np.concatenate([wq[e].T @ xq[:, e * C:(e + 1) * C] for e in range(E)], axis=1)


def setup_inputs():
    n = np.random.standard_normal
    s = mx_kscale(K)[:, None]
    packed = [pack_weight(m) for m in n((E, K, N)) / np.sqrt(K) / s[None]]
    return {
        "xT": (n((K, T)) * s).astype(np.float32),
        "w_words": np.stack([m[0] for m in packed]),
        "w_scales": np.stack([m[1] for m in packed]),
        "b": (0.3 * n((N, E))).astype(np.float32),
        "gate": np.tile(np.random.uniform(0.2, 1.0, E * C), (N, 1)).astype(np.float32),
        "offs": striped(np.random.permutation(T)[:E * C]),
        "dst": striped(np.random.permutation(T)[:E * C]),
    }


def reference(xT, w_words, w_scales, b, gate, offs, dst):
    idx = unstriped(offs)
    w = np.stack([unpack_weight(w_words[e], w_scales[e]) for e in range(E)])
    xq = mxq(f64(xT)[:, idx], 0, "e4m3")
    y = by_expert(w, xq)
    y = relu(y + np.repeat(f64(b), C, axis=1))
    out = np.zeros((N, T))
    out[:, unstriped(dst)] = f64(gate) * y
    return out

@@ -1,0 +1,129 @@
+import concourse.mybir as mybir
+
+F32 = mybir.dt.float32
+BF16 = mybir.dt.bfloat16
+I32 = mybir.dt.int32
+U32 = mybir.dt.uint32
+U16 = mybir.dt.uint16
+U8 = mybir.dt.uint8
+FP8X4 = mybir.dt.float8_e4m3fn_x4
+RELU = mybir.ActivationFunctionType.Relu
+MULT = mybir.AluOpType.mult
+
+P = 128
+PACK = 4
+K = 1024
+T = 512
+E = 4
+C = 128
+N = 128
+PASSES = 2
+FLOPS = 2 * K * N * T
+
+CHUNKS = ((0, 0, 256, 168), (0, 256, 512, 168), (1, 0, 256, 0), (1, 256, 512, 112))
+PLANE = (4, 0)
+
+
+def tile_moe_two_lin_relu_kernel(tc, xT, w_words, w_scales, b, gate, offs, dst, out):
+    nc = tc.nc
+    with tc.tile_pool(name="keep", bufs=1) as keep, tc.psum_pool(name="psum", bufs=1) as psum:
+        offsets = keep.tile([P, T // 16], U16, name="offsets")
+        places = keep.tile([P, T // 16], U16, name="places")
+        warm = keep.tile([P, 1], F32, name="warm")
+        weight_scales = keep.tile([P, E * PASSES, N], U8, name="weight_scales", align_bytes=64)
+        token_scales = keep.tile([P, T], U8, name="token_scales", align_bytes=64)
+        nc.vector.memset(warm[:], 0.0)
+        nc.vector.memset(weight_scales[:].rearrange("p g n -> p (g n)").bitcast(I32), 0)
+        nc.gpsimd.memset(token_scales[:], 0)
+        nc.scalar.activation(warm[:], warm[:], RELU)
+
+        rows = xT.rearrange("(a p j) t -> a p j t", a=PASSES, j=PACK)
+        raw_first = keep.tile([P, PACK, T], F32, name="raw_first")
+        nc.sync.dma_start(raw_first[:], rows[0])
+        nc.sync.dma_start(offsets[:], offs)
+        raws = [raw_first[:, :, 0:256], raw_first[:, :, 256:512]]
+        for h in range(2):
+            raw = keep.tile([P, PACK, 256], F32, name=f"raw{h}")
+            nc.sync.dma_start(raw[:], rows[1][:, :, h * 256 : (h + 1) * 256])
+            raws.append(raw[:])
+        bias = keep.tile([P, E], F32, name="bias")
+        weights = keep.tile([P, E * PASSES, N], U32, name="weights", align_bytes=64)
+        gates = keep.tile([P, E * C], F32, name="gates")
+        scales_in = w_scales.rearrange("e a q n -> q (e a) n").bitcast(I32)
+        for q in range(4):
+            nc.sync.dma_start(
+                weight_scales[32 * q : 32 * q + 4, :, :].bitcast(I32),
+                scales_in[4 * q : 4 * q + 4, :, :],
+            )
+        nc.sync.dma_start(bias[:], b)
+        nc.sync.dma_start(places[:], dst)
+        nc.sync.dma_start(weights[:].bitcast(I32), w_words.rearrange("e a p n r -> p (e a) (n r)").bitcast(I32))
+        nc.sync.dma_start(gates[:], gate)
+
+        words = [keep.tile([P, T], U32, name=f"words{a}", align_bytes=64) for a in range(PASSES)]
+        slot_words = [keep.tile([P, E * C], U32, name=f"slot_words{a}", align_bytes=64) for a in range(PASSES)]
+        slot_scales = keep.tile([P, E * C], U8, name="slot_scales", align_bytes=64)
+        banks = [psum.tile([N, C], F32, name=f"bank{e}") for e in range(E)]
+        results = [keep.tile([N, 2 * C], F32, name=f"result{h}") for h in range(2)]
+        placed = keep.tile([N, T], F32, name="placed")
+
+        def gather_words(a, j0, j1):
+            nc.vector.tensor_copy(slot_words[a][:, j0:j1], words[a][:].indirect(offsets[:, j0 // 16 : j1 // 16]))
+
+        def multiply(e, a):
+            cols = slice(e * C, (e + 1) * C)
+            nc.tensor.matmul_mx(
+                out=banks[e][:],
+                lhsT=weights[:, e * PASSES + a, :].bitcast(FP8X4),
+                lhsT_scale=weight_scales[:, e * PASSES + a, :],
+                rhs=slot_words[a][:, cols].bitcast(FP8X4),
+                rhs_scale=slot_scales[PLANE[a] :, cols],
+                start=(a == 0),
+                stop=(a == PASSES - 1),
+            )
+
+        grouped = [
+            keep.tile([P, t1 - t0, PACK], BF16, name=f"grouped{i}", align_bytes=64)
+            for i, (_, t0, t1, _) in enumerate(CHUNKS)
+        ]
+
+        def interleave(i):
+            _, t0, t1, split = CHUNKS[i]
+            for copy, c0, c1 in ((nc.vector.tensor_copy, 0, split), (nc.scalar.copy, split, t1 - t0)):
+                if c0 < c1:
+                    copy(
+                        grouped[i][:, c0:c1, :].rearrange("p (c i) j -> p c j i", i=4),
+                        raws[i][:, :, c0:c1].rearrange("p j (c i) -> p c j i", i=4),
+                    )
+
+        def quantise(i, c0, c1):
+            a, t0, _, _ = CHUNKS[i]
+            nc.vector.quantize_mx(
+                out=words[a][:, t0 + c0 : t0 + c1].bitcast(FP8X4),
+                scales=token_scales[PLANE[a] :, t0 + c0 : t0 + c1],
+                in_=grouped[i][:, c0:c1, :].rearrange("p t j -> p (t j)"),
+            )
+
+        interleave(0)
+        interleave(1)
+        quantise(0, 0, 256)
+        quantise(1, 0, 256)
+        gather_words(0, 0, 256)
+        gather_words(0, 256, 512)
+        interleave(2)
+        interleave(3)
+        quantise(2, 0, 256)
+        quantise(3, 0, 256)
+        for h in range(2):
+            j0, j1 = 2 * h * C, 2 * (h + 1) * C
+            nc.vector.tensor_copy(slot_scales[:, j0:j1], token_scales[:].indirect(offsets[:, j0 // 16 : j1 // 16]))
+            gather_words(1, j0, j1)
+            for e in (2 * h, 2 * h + 1):
+                multiply(e, 0)
+            for e in (2 * h, 2 * h + 1):
+                multiply(e, 1)
+                nc.scalar.activation(results[h][:, (e % 2) * C : (e % 2 + 1) * C], banks[e][:], RELU, bias=bias[:, e : e + 1])
+        for h in range(2):
+            j0, j1 = 2 * h * C, 2 * (h + 1) * C
+            nc.vector.tensor_tensor(placed[:].indirect(places[:, j0 // 16 : j1 // 16]), results[h][:], gates[:, j0:j1], MULT)
+        nc.sync.dma_start(out, placed[:])

@@ -47,7 +47,7 @@ def tile_moe_two_lin_relu_kernel(tc, xT, w_words, w_scales, b, gate, offs, dst, 
             nc.sync.dma_start(raw[:], rows[1][:, :, h * 256 : (h + 1) * 256])
             raws.append(raw[:])
         bias = keep.tile([P, E], F32, name="bias")
-        weights = keep.tile([P, E * PASSES, N], U32, name="weights", align_bytes=64)
+        weights = [keep.tile([P, E, N], U32, name=f"weights{h}", align_bytes=64) for h in range(2)]
         gates = keep.tile([P, E * C], F32, name="gates")
         scales_in = w_scales.rearrange("e a q n -> q (e a) n").bitcast(I32)
         for q in range(4):
@@ -55,9 +55,11 @@ def tile_moe_two_lin_relu_kernel(tc, xT, w_words, w_scales, b, gate, offs, dst, 
                 weight_scales[32 * q : 32 * q + 4, :, :].bitcast(I32),
                 scales_in[4 * q : 4 * q + 4, :, :],
             )
+        words_in = w_words.rearrange("e a p n r -> p (e a) (n r)").bitcast(I32)
+        for h in range(2):
+            nc.sync.dma_start(weights[h][:].bitcast(I32), words_in[:, h * E : (h + 1) * E, :])
         nc.sync.dma_start(bias[:], b)
         nc.sync.dma_start(places[:], dst)
-        nc.sync.dma_start(weights[:].bitcast(I32), w_words.rearrange("e a p n r -> p (e a) (n r)").bitcast(I32))
         nc.sync.dma_start(gates[:], gate)
 
         words = [keep.tile([P, T], U32, name=f"words{a}", align_bytes=64) for a in range(PASSES)]
@@ -74,7 +76,7 @@ def tile_moe_two_lin_relu_kernel(tc, xT, w_words, w_scales, b, gate, offs, dst, 
             cols = slice(e * C, (e + 1) * C)
             nc.tensor.matmul_mx(
                 out=banks[e][:],
-                lhsT=weights[:, e * PASSES + a, :].bitcast(FP8X4),
+                lhsT=weights[e // 2][:, (e % 2) * PASSES + a, :].bitcast(FP8X4),
                 lhsT_scale=weight_scales[:, e * PASSES + a, :],
                 rhs=slot_words[a][:, cols].bitcast(FP8X4),
                 rhs_scale=slot_scales[PLANE[a] :, cols],

@@ -20,7 +20,8 @@ N = 128
 PASSES = 2
 FLOPS = 2 * K * N * T
 
-CHUNKS = ((0, 0, 256, 168), (0, 256, 512, 168), (1, 0, 256, 0), (1, 256, 512, 112))
+LOADS = ((1, 0, 256), (1, 256, 512))
+UNITS = ((0, 0, 256), (0, 256, 512), (1, 0, 256), (1, 256, 512))
 PLANE = (4, 0)
 
 
@@ -38,14 +39,17 @@ def tile_moe_two_lin_relu_kernel(tc, xT, w_words, w_scales, b, gate, offs, dst, 
         nc.scalar.activation(warm[:], warm[:], RELU)
 
         rows = xT.rearrange("(a p j) t -> a p j t", a=PASSES, j=PACK)
-        raw_first = keep.tile([P, PACK, T], F32, name="raw_first")
-        nc.sync.dma_start(raw_first[:], rows[0])
+        pairs = []
+        for u in range(2):
+            pair = keep.tile([P, 2, T], F32, name=f"pair{u}")
+            nc.sync.dma_start(pair[:], rows[0][:, 2 * u : 2 * u + 2, :])
+            pairs.append(pair)
         nc.sync.dma_start(offsets[:], offs)
-        raws = [raw_first[:, :, 0:256], raw_first[:, :, 256:512]]
-        for h in range(2):
-            raw = keep.tile([P, PACK, 256], F32, name=f"raw{h}")
-            nc.sync.dma_start(raw[:], rows[1][:, :, h * 256 : (h + 1) * 256])
-            raws.append(raw[:])
+        raws = []
+        for i, (a, t0, t1) in enumerate(LOADS):
+            raw = keep.tile([P, PACK, t1 - t0], F32, name=f"raw{i}", tag=f"raw{i}", align_bytes=64)
+            nc.sync.dma_start(raw[:], rows[a][:, :, t0:t1])
+            raws.append(raw)
         bias = keep.tile([P, E], F32, name="bias")
         weights = [keep.tile([P, E, N], U32, name=f"weights{h}", align_bytes=64) for h in range(2)]
         gates = keep.tile([P, E * C], F32, name="gates")
@@ -63,69 +67,99 @@ def tile_moe_two_lin_relu_kernel(tc, xT, w_words, w_scales, b, gate, offs, dst, 
         nc.sync.dma_start(gates[:], gate)
 
         words = [keep.tile([P, T], U32, name=f"words{a}", align_bytes=64) for a in range(PASSES)]
-        slot_words = [keep.tile([P, E * C], U32, name=f"slot_words{a}", align_bytes=64) for a in range(PASSES)]
         slot_scales = keep.tile([P, E * C], U8, name="slot_scales", align_bytes=64)
         banks = [psum.tile([N, C], F32, name=f"bank{e}") for e in range(E)]
         results = [keep.tile([N, 2 * C], F32, name=f"result{h}") for h in range(2)]
         placed = keep.tile([N, T], F32, name="placed")
+        grouped = [
+            keep.tile([P, t1 - t0, PACK], BF16, name=f"grouped{i}", tag=f"grouped{i}", align_bytes=64)
+            for i, (_, t0, t1) in enumerate(UNITS)
+        ]
+        slot_words = {}
 
-        def gather_words(a, j0, j1):
-            nc.vector.tensor_copy(slot_words[a][:, j0:j1], words[a][:].indirect(offsets[:, j0 // 16 : j1 // 16]))
+        def gather_words(a, e0, e1, tag=None):
+            name = f"slot_words{a}_{e0}"
+            tile = keep.tile([P, (e1 - e0) * C], U32, name=name, tag=tag or name, align_bytes=64)
+            nc.vector.tensor_copy(tile[:], words[a][:].indirect(offsets[:, e0 * C // 16 : e1 * C // 16]))
+            for e in range(e0, e1):
+                slot_words[a, e] = tile[:, (e - e0) * C : (e - e0 + 1) * C]
+
+        def gather_scales(e0, e1):
+            window = token_scales[:].indirect(offsets[:, e0 * C // 16 : e1 * C // 16])
+            nc.vector.tensor_copy(slot_scales[:, e0 * C : e1 * C], window)
 
         def multiply(e, a):
-            cols = slice(e * C, (e + 1) * C)
             nc.tensor.matmul_mx(
                 out=banks[e][:],
                 lhsT=weights[e // 2][:, (e % 2) * PASSES + a, :].bitcast(FP8X4),
                 lhsT_scale=weight_scales[:, e * PASSES + a, :],
-                rhs=slot_words[a][:, cols].bitcast(FP8X4),
-                rhs_scale=slot_scales[PLANE[a] :, cols],
+                rhs=slot_words[a, e].bitcast(FP8X4),
+                rhs_scale=slot_scales[PLANE[a] :, e * C : (e + 1) * C],
                 start=(a == 0),
                 stop=(a == PASSES - 1),
             )
 
-        grouped = [
-            keep.tile([P, t1 - t0, PACK], BF16, name=f"grouped{i}", align_bytes=64)
-            for i, (_, t0, t1, _) in enumerate(CHUNKS)
-        ]
+        def finish(e):
+            multiply(e, 1)
+            nc.scalar.activation(results[e // 2][:, (e % 2) * C : (e % 2 + 1) * C], banks[e][:], RELU, bias=bias[:, e : e + 1])
 
-        def interleave(i):
-            _, t0, t1, split = CHUNKS[i]
-            for copy, c0, c1 in ((nc.vector.tensor_copy, 0, split), (nc.scalar.copy, split, t1 - t0)):
-                if c0 < c1:
-                    copy(
-                        grouped[i][:, c0:c1, :].rearrange("p (c i) j -> p c j i", i=4),
-                        raws[i][:, :, c0:c1].rearrange("p j (c i) -> p c j i", i=4),
-                    )
-
-        def quantise(i, c0, c1):
-            a, t0, _, _ = CHUNKS[i]
-            nc.vector.quantize_mx(
-                out=words[a][:, t0 + c0 : t0 + c1].bitcast(FP8X4),
-                scales=token_scales[PLANE[a] :, t0 + c0 : t0 + c1],
-                in_=grouped[i][:, c0:c1, :].rearrange("p t j -> p (t j)"),
-            )
-
-        interleave(0)
-        interleave(1)
-        quantise(0, 0, 256)
-        quantise(1, 0, 256)
-        gather_words(0, 0, 256)
-        gather_words(0, 256, 512)
-        interleave(2)
-        interleave(3)
-        quantise(2, 0, 256)
-        quantise(3, 0, 256)
-        for h in range(2):
-            j0, j1 = 2 * h * C, 2 * (h + 1) * C
-            nc.vector.tensor_copy(slot_scales[:, j0:j1], token_scales[:].indirect(offsets[:, j0 // 16 : j1 // 16]))
-            gather_words(1, j0, j1)
-            for e in (2 * h, 2 * h + 1):
-                multiply(e, 0)
-            for e in (2 * h, 2 * h + 1):
-                multiply(e, 1)
-                nc.scalar.activation(results[h][:, (e % 2) * C : (e % 2 + 1) * C], banks[e][:], RELU, bias=bias[:, e : e + 1])
-        for h in range(2):
+        def scatter(h):
             j0, j1 = 2 * h * C, 2 * (h + 1) * C
             nc.vector.tensor_tensor(placed[:].indirect(places[:, j0 // 16 : j1 // 16]), results[h][:], gates[:, j0:j1], MULT)
+
+        def interleave(copy, a, c0, c1):
+            (load,) = [i for i, (x, t0, t1) in enumerate(LOADS) if x == a and t0 <= c0 and c1 <= t1]
+            (unit,) = [i for i, (x, t0, t1) in enumerate(UNITS) if x == a and t0 <= c0 and c1 <= t1]
+            g0, r0 = UNITS[unit][1], LOADS[load][1]
+            copy(
+                grouped[unit][:, c0 - g0 : c1 - g0, :].rearrange("p (c i) j -> p c j i", i=4),
+                raws[load][:, :, c0 - r0 : c1 - r0].rearrange("p j (c i) -> p c j i", i=4),
+            )
+
+        def place_pair(copy, u, c0, c1):
+            unit = c0 // 256
+            g0 = UNITS[unit][1]
+            copy(
+                grouped[unit][:, c0 - g0 : c1 - g0, 2 * u : 2 * u + 2],
+                pairs[u][:, :, c0:c1].rearrange("p j t -> p t j"),
+            )
+
+        def quantise(unit):
+            a, t0, t1 = UNITS[unit]
+            nc.vector.quantize_mx(
+                out=words[a][:, t0:t1].bitcast(FP8X4),
+                scales=token_scales[PLANE[a] :, t0:t1],
+                in_=grouped[unit][:].rearrange("p t j -> p (t j)"),
+            )
+
+        vector, scalar = nc.vector.tensor_copy, nc.scalar.copy
+        place_pair(vector, 0, 0, 256)
+        place_pair(vector, 0, 256, 512)
+        place_pair(vector, 1, 0, 256)
+        place_pair(vector, 1, 256, 352)
+        place_pair(scalar, 1, 352, 512)
+        quantise(0)
+        quantise(1)
+        gather_words(0, 0, 2)
+        gather_words(0, 2, 3)
+        interleave(scalar, 1, 0, 256)
+        interleave(vector, 1, 256, 384)
+        interleave(scalar, 1, 384, 512)
+        quantise(2)
+        quantise(3)
+        gather_words(0, 3, 4, tag="raw1")
+        gather_scales(0, 2)
+        gather_words(1, 0, 2)
+        multiply(0, 0)
+        multiply(1, 0)
+        finish(0)
+        finish(1)
+        gather_scales(2, 4)
+        gather_words(1, 2, 4)
+        multiply(2, 0)
+        multiply(3, 0)
+        finish(2)
+        finish(3)
+        scatter(0)
+        scatter(1)
         nc.sync.dma_start(out, placed[:])

@@ -52,19 +52,30 @@ def tile_moe_two_lin_relu_kernel(tc, xT, w_words, w_scales, b, gate, offs, dst, 
             raws.append(raw)
         bias = keep.tile([P, E], F32, name="bias")
         weights = [keep.tile([P, E, N], U32, name=f"weights{h}", align_bytes=64) for h in range(2)]
-        gates = keep.tile([P, E * C], F32, name="gates")
+        gates = [keep.tile([P, 2 * C], F32, name=f"gates{h}") for h in range(2)]
         scales_in = w_scales.rearrange("e a q n -> q (e a) n").bitcast(I32)
-        for q in range(4):
-            nc.sync.dma_start(
-                weight_scales[32 * q : 32 * q + 4, :, :].bitcast(I32),
-                scales_in[4 * q : 4 * q + 4, :, :],
-            )
         words_in = w_words.rearrange("e a p n r -> p (e a) (n r)").bitcast(I32)
-        for h in range(2):
+
+        def load_scales():
+            for q in range(4):
+                nc.sync.dma_start(
+                    weight_scales[32 * q : 32 * q + 4, :, :].bitcast(I32),
+                    scales_in[4 * q : 4 * q + 4, :, :],
+                )
+
+        def load_weights(h):
             nc.sync.dma_start(weights[h][:].bitcast(I32), words_in[:, h * E : (h + 1) * E, :])
+
+        def load_gates(h):
+            nc.sync.dma_start(gates[h][:], gate[:, 2 * h * C : 2 * (h + 1) * C])
+
         nc.sync.dma_start(bias[:], b)
+        load_scales()
+        load_weights(0)
+        load_gates(0)
         nc.sync.dma_start(places[:], dst)
-        nc.sync.dma_start(gates[:], gate)
+        load_weights(1)
+        load_gates(1)
 
         words = [keep.tile([P, T], U32, name=f"words{a}", align_bytes=64) for a in range(PASSES)]
         slot_scales = keep.tile([P, E * C], U8, name="slot_scales", align_bytes=64)
@@ -105,7 +116,7 @@ def tile_moe_two_lin_relu_kernel(tc, xT, w_words, w_scales, b, gate, offs, dst, 
 
         def scatter(h):
             j0, j1 = 2 * h * C, 2 * (h + 1) * C
-            nc.vector.tensor_tensor(placed[:].indirect(places[:, j0 // 16 : j1 // 16]), results[h][:], gates[:, j0:j1], MULT)
+            nc.vector.tensor_tensor(placed[:].indirect(places[:, j0 // 16 : j1 // 16]), results[h][:], gates[h][:], MULT)
 
         def interleave(copy, a, c0, c1):
             (load,) = [i for i, (x, t0, t1) in enumerate(LOADS) if x == a and t0 <= c0 and c1 <= t1]

@@ -77,7 +77,8 @@ def tile_moe_two_lin_relu_kernel(tc, xT, w_words, w_scales, b, gate, offs, dst, 
         load_weights(1)
         load_gates(1)
 
-        words = [keep.tile([P, T], U32, name=f"words{a}", align_bytes=64) for a in range(PASSES)]
+        words = [keep.tile([P, width], U32, name=f"words{a}", align_bytes=64) for a, width in enumerate((T + 192, T))]
+        nc.vector.memset(words[0][:, T:].bitcast(I32), 0)
         slot_scales = keep.tile([P, E * C], U8, name="slot_scales", align_bytes=64)
         banks = [psum.tile([N, C], F32, name=f"bank{e}") for e in range(E)]
         results = [keep.tile([N, 2 * C], F32, name=f"result{h}") for h in range(2)]
@@ -147,23 +148,22 @@ def tile_moe_two_lin_relu_kernel(tc, xT, w_words, w_scales, b, gate, offs, dst, 
         place_pair(vector, 0, 0, 256)
         place_pair(vector, 0, 256, 512)
         place_pair(vector, 1, 0, 256)
-        place_pair(vector, 1, 256, 352)
-        place_pair(scalar, 1, 352, 512)
+        place_pair(vector, 1, 256, 320)
+        place_pair(scalar, 1, 320, 512)
         quantise(0)
         quantise(1)
-        gather_words(0, 0, 2)
-        gather_words(0, 2, 3)
+        gather_words(0, 0, 4)
         interleave(scalar, 1, 0, 256)
         interleave(vector, 1, 256, 384)
         interleave(scalar, 1, 384, 512)
         quantise(2)
         quantise(3)
-        gather_words(0, 3, 4, tag="raw1")
         gather_scales(0, 2)
-        gather_words(1, 0, 2)
+        gather_words(1, 0, 1)
         multiply(0, 0)
         multiply(1, 0)
         finish(0)
+        gather_words(1, 1, 2)
         finish(1)
         gather_scales(2, 4)
         gather_words(1, 2, 4)

@@ -30,13 +30,10 @@ def tile_moe_two_lin_relu_kernel(tc, xT, w_words, w_scales, b, gate, offs, dst, 
     with tc.tile_pool(name="keep", bufs=1) as keep, tc.psum_pool(name="psum", bufs=1) as psum:
         offsets = keep.tile([P, T // 16], U16, name="offsets")
         places = keep.tile([P, T // 16], U16, name="places")
-        warm = keep.tile([P, 1], F32, name="warm")
         weight_scales = keep.tile([P, E * PASSES, N], U8, name="weight_scales", align_bytes=64)
         token_scales = keep.tile([P, T], U8, name="token_scales", align_bytes=64)
-        nc.vector.memset(warm[:], 0.0)
         nc.vector.memset(weight_scales[:].rearrange("p g n -> p (g n)").bitcast(I32), 0)
         nc.gpsimd.memset(token_scales[:], 0)
-        nc.scalar.activation(warm[:], warm[:], RELU)
 
         rows = xT.rearrange("(a p j) t -> a p j t", a=PASSES, j=PACK)
         pairs = []
@@ -124,8 +121,8 @@ def tile_moe_two_lin_relu_kernel(tc, xT, w_words, w_scales, b, gate, offs, dst, 
             (unit,) = [i for i, (x, t0, t1) in enumerate(UNITS) if x == a and t0 <= c0 and c1 <= t1]
             g0, r0 = UNITS[unit][1], LOADS[load][1]
             copy(
-                grouped[unit][:, c0 - g0 : c1 - g0, :].rearrange("p (c i) j -> p c j i", i=4),
-                raws[load][:, :, c0 - r0 : c1 - r0].rearrange("p j (c i) -> p c j i", i=4),
+                grouped[unit][:, c0 - g0 : c1 - g0, :].rearrange("p (c i) j -> p c j i", i=2),
+                raws[load][:, :, c0 - r0 : c1 - r0].rearrange("p j (c i) -> p c j i", i=2),
             )
 
         def place_pair(copy, u, c0, c1):

@@ -20,8 +20,7 @@ N = 128
 PASSES = 2
 FLOPS = 2 * K * N * T
 
-LOADS = ((1, 0, 256), (1, 256, 512))
-UNITS = ((0, 0, 256), (0, 256, 512), (1, 0, 256), (1, 256, 512))
+HALF = T // 2
 PLANE = (4, 0)
 
 
@@ -36,17 +35,14 @@ def tile_moe_two_lin_relu_kernel(tc, xT, w_words, w_scales, b, gate, offs, dst, 
         nc.gpsimd.memset(token_scales[:], 0)
 
         rows = xT.rearrange("(a p j) t -> a p j t", a=PASSES, j=PACK)
-        pairs = []
-        for u in range(2):
-            pair = keep.tile([P, 2, T], F32, name=f"pair{u}")
-            nc.sync.dma_start(pair[:], rows[0][:, 2 * u : 2 * u + 2, :])
-            pairs.append(pair)
-        nc.sync.dma_start(offsets[:], offs)
         raws = []
-        for i, (a, t0, t1) in enumerate(LOADS):
-            raw = keep.tile([P, PACK, t1 - t0], F32, name=f"raw{i}", tag=f"raw{i}", align_bytes=64)
-            nc.sync.dma_start(raw[:], rows[a][:, :, t0:t1])
+        for a in range(PASSES):
+            raw = keep.tile([P, PACK, T], F32, name=f"raw{a}", tag=f"raw{a}", align_bytes=64)
+            for u in range(2):
+                nc.sync.dma_start(raw[:, 2 * u : 2 * u + 2, :], rows[a][:, 2 * u : 2 * u + 2, :])
             raws.append(raw)
+            if a == 0:
+                nc.sync.dma_start(offsets[:], offs)
         bias = keep.tile([P, E], F32, name="bias")
         weights = [keep.tile([P, E, N], U32, name=f"weights{h}", align_bytes=64) for h in range(2)]
         gates = [keep.tile([P, 2 * C], F32, name=f"gates{h}") for h in range(2)]
@@ -74,16 +70,12 @@ def tile_moe_two_lin_relu_kernel(tc, xT, w_words, w_scales, b, gate, offs, dst, 
         load_weights(1)
         load_gates(1)
 
-        words = [keep.tile([P, width], U32, name=f"words{a}", align_bytes=64) for a, width in enumerate((T + 192, T))]
-        nc.vector.memset(words[0][:, T:].bitcast(I32), 0)
+        words = [keep.tile([P, T], U32, name=f"words{a}", align_bytes=64) for a in range(PASSES)]
         slot_scales = keep.tile([P, E * C], U8, name="slot_scales", align_bytes=64)
         banks = [psum.tile([N, C], F32, name=f"bank{e}") for e in range(E)]
         results = [keep.tile([N, 2 * C], F32, name=f"result{h}") for h in range(2)]
         placed = keep.tile([N, T], F32, name="placed")
-        grouped = [
-            keep.tile([P, t1 - t0, PACK], BF16, name=f"grouped{i}", tag=f"grouped{i}", align_bytes=64)
-            for i, (_, t0, t1) in enumerate(UNITS)
-        ]
+        grouped = [keep.tile([P, T, PACK], BF16, name=f"grouped{a}", align_bytes=64) for a in range(PASSES)]
         slot_words = {}
 
         def gather_words(a, e0, e1, tag=None):
@@ -116,45 +108,42 @@ def tile_moe_two_lin_relu_kernel(tc, xT, w_words, w_scales, b, gate, offs, dst, 
             j0, j1 = 2 * h * C, 2 * (h + 1) * C
             nc.vector.tensor_tensor(placed[:].indirect(places[:, j0 // 16 : j1 // 16]), results[h][:], gates[h][:], MULT)
 
-        def interleave(copy, a, c0, c1):
-            (load,) = [i for i, (x, t0, t1) in enumerate(LOADS) if x == a and t0 <= c0 and c1 <= t1]
-            (unit,) = [i for i, (x, t0, t1) in enumerate(UNITS) if x == a and t0 <= c0 and c1 <= t1]
-            g0, r0 = UNITS[unit][1], LOADS[load][1]
+        def place_pair(copy, a, u, c0, c1):
             copy(
-                grouped[unit][:, c0 - g0 : c1 - g0, :].rearrange("p (c i) j -> p c j i", i=2),
-                raws[load][:, :, c0 - r0 : c1 - r0].rearrange("p j (c i) -> p c j i", i=2),
+                grouped[a][:, c0:c1, 2 * u : 2 * u + 2],
+                raws[a][:, 2 * u : 2 * u + 2, c0:c1].rearrange("p j t -> p t j"),
             )
 
-        def place_pair(copy, u, c0, c1):
-            unit = c0 // 256
-            g0 = UNITS[unit][1]
+        def place_all(copy, a, c0, c1):
             copy(
-                grouped[unit][:, c0 - g0 : c1 - g0, 2 * u : 2 * u + 2],
-                pairs[u][:, :, c0:c1].rearrange("p j t -> p t j"),
+                grouped[a][:, c0:c1, :].rearrange("p (c i) j -> p c j i", i=2),
+                raws[a][:, :, c0:c1].rearrange("p j (c i) -> p c j i", i=2),
             )
 
-        def quantise(unit):
-            a, t0, t1 = UNITS[unit]
+        def quantise(a, t0, t1):
             nc.vector.quantize_mx(
                 out=words[a][:, t0:t1].bitcast(FP8X4),
                 scales=token_scales[PLANE[a] :, t0:t1],
-                in_=grouped[unit][:].rearrange("p t j -> p (t j)"),
+                in_=grouped[a][:, t0:t1, :].rearrange("p t j -> p (t j)"),
             )
 
         vector, scalar = nc.vector.tensor_copy, nc.scalar.copy
-        place_pair(vector, 0, 0, 256)
-        place_pair(vector, 0, 256, 512)
-        place_pair(vector, 1, 0, 256)
-        place_pair(vector, 1, 256, 320)
-        place_pair(scalar, 1, 320, 512)
-        quantise(0)
-        quantise(1)
-        gather_words(0, 0, 4)
-        interleave(scalar, 1, 0, 256)
-        interleave(vector, 1, 256, 384)
-        interleave(scalar, 1, 384, 512)
-        quantise(2)
-        quantise(3)
+        place_pair(vector, 0, 0, 0, 352)
+        place_pair(scalar, 0, 0, 352, T)
+        for g0 in (0, HALF):
+            place_pair(vector, 0, 1, g0, g0 + 160)
+            place_pair(scalar, 0, 1, g0 + 160, g0 + HALF)
+        quantise(0, 0, HALF)
+        quantise(0, HALF, T)
+        gather_words(0, 0, 3)
+        place_pair(scalar, 1, 0, 0, HALF)
+        place_pair(scalar, 1, 0, HALF, 352)
+        place_pair(vector, 1, 1, 0, HALF)
+        place_pair(vector, 1, 1, HALF, 352)
+        place_all(scalar, 1, 352, T)
+        quantise(1, 0, HALF)
+        quantise(1, HALF, T)
+        gather_words(0, 3, 4, tag="raw1")
         gather_scales(0, 2)
         gather_words(1, 0, 1)
         multiply(0, 0)

@@ -40,9 +40,9 @@ def tile_moe_two_lin_relu_kernel(tc, xT, w_words, w_scales, b, gate, offs, dst, 
             raw = keep.tile([P, PACK, T], F32, name=f"raw{a}", tag=f"raw{a}", align_bytes=64)
             for u in range(2):
                 nc.sync.dma_start(raw[:, 2 * u : 2 * u + 2, :], rows[a][:, 2 * u : 2 * u + 2, :])
+                if (a, u) == (1, 0):
+                    nc.sync.dma_start(offsets[:], offs)
             raws.append(raw)
-            if a == 0:
-                nc.sync.dma_start(offsets[:], offs)
         bias = keep.tile([P, E], F32, name="bias")
         weights = [keep.tile([P, E, N], U32, name=f"weights{h}", align_bytes=64) for h in range(2)]
         gates = [keep.tile([P, 2 * C], F32, name=f"gates{h}") for h in range(2)]
@@ -135,12 +135,13 @@ def tile_moe_two_lin_relu_kernel(tc, xT, w_words, w_scales, b, gate, offs, dst, 
             place_pair(scalar, 0, 1, g0 + 160, g0 + HALF)
         quantise(0, 0, HALF)
         quantise(0, HALF, T)
+        place_pair(vector, 1, 0, 384, T)
         gather_words(0, 0, 3)
         place_pair(scalar, 1, 0, 0, HALF)
-        place_pair(scalar, 1, 0, HALF, 352)
-        place_pair(vector, 1, 1, 0, HALF)
-        place_pair(vector, 1, 1, HALF, 352)
-        place_all(scalar, 1, 352, T)
+        place_pair(scalar, 1, 0, HALF, 384)
+        for g0 in (0, HALF):
+            place_pair(vector, 1, 1, g0, g0 + 160)
+            place_pair(scalar, 1, 1, g0 + 160, g0 + HALF)
         quantise(1, 0, HALF)
         quantise(1, HALF, T)
         gather_words(0, 3, 4, tag="raw1")

@@ -32,7 +32,7 @@ def tile_moe_two_lin_relu_kernel(tc, xT, w_words, w_scales, b, gate, offs, dst, 
         weight_scales = keep.tile([P, E * PASSES, N], U8, name="weight_scales", align_bytes=64)
         token_scales = keep.tile([P, T], U8, name="token_scales", align_bytes=64)
         nc.vector.memset(weight_scales[:].rearrange("p g n -> p (g n)").bitcast(I32), 0)
-        nc.gpsimd.memset(token_scales[:], 0)
+        nc.vector.memset(token_scales[:].bitcast(I32), 0)
 
         rows = xT.rearrange("(a p j) t -> a p j t", a=PASSES, j=PACK)
         raws = []
@@ -128,20 +128,22 @@ def tile_moe_two_lin_relu_kernel(tc, xT, w_words, w_scales, b, gate, offs, dst, 
             )
 
         vector, scalar = nc.vector.tensor_copy, nc.scalar.copy
+
+        def share_second_pair(a):
+            for g0, split in ((0, 176), (HALF, 160)):
+                place_pair(vector, a, 1, g0, g0 + split)
+                place_pair(scalar, a, 1, g0 + split, g0 + HALF)
+
         place_pair(vector, 0, 0, 0, 352)
         place_pair(scalar, 0, 0, 352, T)
-        for g0 in (0, HALF):
-            place_pair(vector, 0, 1, g0, g0 + 160)
-            place_pair(scalar, 0, 1, g0 + 160, g0 + HALF)
+        share_second_pair(0)
         quantise(0, 0, HALF)
         quantise(0, HALF, T)
-        place_pair(vector, 1, 0, 384, T)
+        place_pair(vector, 1, 0, 368, T)
         gather_words(0, 0, 3)
         place_pair(scalar, 1, 0, 0, HALF)
-        place_pair(scalar, 1, 0, HALF, 384)
-        for g0 in (0, HALF):
-            place_pair(vector, 1, 1, g0, g0 + 160)
-            place_pair(scalar, 1, 1, g0 + 160, g0 + HALF)
+        place_pair(scalar, 1, 0, HALF, 368)
+        share_second_pair(1)
         quantise(1, 0, HALF)
         quantise(1, HALF, T)
         gather_words(0, 3, 4, tag="raw1")

@@ -45,7 +45,7 @@ def tile_moe_two_lin_relu_kernel(tc, xT, w_words, w_scales, b, gate, offs, dst, 
             raws.append(raw)
         bias = keep.tile([P, E], F32, name="bias")
         weights = [keep.tile([P, E, N], U32, name=f"weights{h}", align_bytes=64) for h in range(2)]
-        gates = [keep.tile([P, 2 * C], F32, name=f"gates{h}") for h in range(2)]
+        gates = keep.tile([P, T], F32, name="gates")
         scales_in = w_scales.rearrange("e a q n -> q (e a) n").bitcast(I32)
         words_in = w_words.rearrange("e a p n r -> p (e a) (n r)").bitcast(I32)
 
@@ -59,16 +59,12 @@ def tile_moe_two_lin_relu_kernel(tc, xT, w_words, w_scales, b, gate, offs, dst, 
         def load_weights(h):
             nc.sync.dma_start(weights[h][:].bitcast(I32), words_in[:, h * E : (h + 1) * E, :])
 
-        def load_gates(h):
-            nc.sync.dma_start(gates[h][:], gate[:, 2 * h * C : 2 * (h + 1) * C])
-
         nc.sync.dma_start(bias[:], b)
         load_scales()
         load_weights(0)
-        load_gates(0)
+        nc.sync.dma_start(gates[:], gate)
         nc.sync.dma_start(places[:], dst)
         load_weights(1)
-        load_gates(1)
 
         words = [keep.tile([P, T], U32, name=f"words{a}", align_bytes=64) for a in range(PASSES)]
         slot_scales = keep.tile([P, E * C], U8, name="slot_scales", align_bytes=64)
@@ -106,7 +102,7 @@ def tile_moe_two_lin_relu_kernel(tc, xT, w_words, w_scales, b, gate, offs, dst, 
 
         def scatter(h):
             j0, j1 = 2 * h * C, 2 * (h + 1) * C
-            nc.vector.tensor_tensor(placed[:].indirect(places[:, j0 // 16 : j1 // 16]), results[h][:], gates[h][:], MULT)
+            nc.vector.tensor_tensor(placed[:].indirect(places[:, j0 // 16 : j1 // 16]), results[h][:], gates[:, j0:j1], MULT)
 
         def place_pair(copy, a, u, c0, c1):
             copy(
@@ -160,6 +156,7 @@ def tile_moe_two_lin_relu_kernel(tc, xT, w_words, w_scales, b, gate, offs, dst, 
         multiply(3, 0)
         finish(2)
         finish(3)
+        nc.sync.dma_start(out[:, 0:8], results[0][:, 0:8])
         scatter(0)
         scatter(1)
         nc.sync.dma_start(out, placed[:])

@@ -44,7 +44,7 @@ def tile_moe_two_lin_relu_kernel(tc, xT, w_words, w_scales, b, gate, offs, dst, 
                     nc.sync.dma_start(offsets[:], offs)
             raws.append(raw)
         bias = keep.tile([P, E], F32, name="bias")
-        weights = [keep.tile([P, E, N], U32, name=f"weights{h}", align_bytes=64) for h in range(2)]
+        weights = {}
         gates = keep.tile([P, T], F32, name="gates")
         scales_in = w_scales.rearrange("e a q n -> q (e a) n").bitcast(I32)
         words_in = w_words.rearrange("e a p n r -> p (e a) (n r)").bitcast(I32)
@@ -56,15 +56,20 @@ def tile_moe_two_lin_relu_kernel(tc, xT, w_words, w_scales, b, gate, offs, dst, 
                     scales_in[4 * q : 4 * q + 4, :, :],
                 )
 
-        def load_weights(h):
-            nc.sync.dma_start(weights[h][:].bitcast(I32), words_in[:, h * E : (h + 1) * E, :])
+        def load_weights(e0, e1):
+            tile = keep.tile([P, (e1 - e0) * PASSES, N], U32, name=f"weights{e0}", align_bytes=64)
+            nc.sync.dma_start(tile[:].bitcast(I32), words_in[:, e0 * PASSES : e1 * PASSES, :])
+            for e in range(e0, e1):
+                for a in range(PASSES):
+                    weights[e, a] = tile[:, (e - e0) * PASSES + a, :]
 
         nc.sync.dma_start(bias[:], b)
         load_scales()
-        load_weights(0)
-        nc.sync.dma_start(gates[:], gate)
+        load_weights(0, 1)
+        load_weights(1, 2)
         nc.sync.dma_start(places[:], dst)
-        load_weights(1)
+        nc.sync.dma_start(gates[:], gate)
+        load_weights(2, 4)
 
         words = [keep.tile([P, T], U32, name=f"words{a}", align_bytes=64) for a in range(PASSES)]
         slot_scales = keep.tile([P, E * C], U8, name="slot_scales", align_bytes=64)
@@ -88,7 +93,7 @@ def tile_moe_two_lin_relu_kernel(tc, xT, w_words, w_scales, b, gate, offs, dst, 
         def multiply(e, a):
             nc.tensor.matmul_mx(
                 out=banks[e][:],
-                lhsT=weights[e // 2][:, (e % 2) * PASSES + a, :].bitcast(FP8X4),
+                lhsT=weights[e, a].bitcast(FP8X4),
                 lhsT_scale=weight_scales[:, e * PASSES + a, :],
                 rhs=slot_words[a, e].bitcast(FP8X4),
                 rhs_scale=slot_scales[PLANE[a] :, e * C : (e + 1) * C],
@@ -146,8 +151,8 @@ def tile_moe_two_lin_relu_kernel(tc, xT, w_words, w_scales, b, gate, offs, dst, 
         gather_scales(0, 2)
         gather_words(1, 0, 1)
         multiply(0, 0)
-        multiply(1, 0)
         finish(0)
+        multiply(1, 0)
         gather_words(1, 1, 2)
         finish(1)
         gather_scales(2, 4)
@@ -156,7 +161,6 @@ def tile_moe_two_lin_relu_kernel(tc, xT, w_words, w_scales, b, gate, offs, dst, 
         multiply(3, 0)
         finish(2)
         finish(3)
-        nc.sync.dma_start(out[:, 0:8], results[0][:, 0:8])
         scatter(0)
         scatter(1)
         nc.sync.dma_start(out, placed[:])

@@ -29,15 +29,15 @@ def tile_moe_two_lin_relu_kernel(tc, xT, w_words, w_scales, b, gate, offs, dst, 
     with tc.tile_pool(name="keep", bufs=1) as keep, tc.psum_pool(name="psum", bufs=1) as psum:
         offsets = keep.tile([P, T // 16], U16, name="offsets")
         places = keep.tile([P, T // 16], U16, name="places")
-        weight_scales = keep.tile([P, E * PASSES, N], U8, name="weight_scales", align_bytes=64)
-        token_scales = keep.tile([P, T], U8, name="token_scales", align_bytes=64)
+        weight_scales = keep.tile([P, E * PASSES, N], U8, name="weight_scales", align_bytes=256)
+        token_scales = keep.tile([P, T], U8, name="token_scales", align_bytes=256)
         nc.vector.memset(weight_scales[:].rearrange("p g n -> p (g n)").bitcast(I32), 0)
         nc.vector.memset(token_scales[:].bitcast(I32), 0)
 
         rows = xT.rearrange("(a p j) t -> a p j t", a=PASSES, j=PACK)
         raws = []
         for a in range(PASSES):
-            raw = keep.tile([P, PACK, T], F32, name=f"raw{a}", tag=f"raw{a}", align_bytes=64)
+            raw = keep.tile([P, PACK, T], F32, name=f"raw{a}", tag=f"raw{a}", align_bytes=256)
             for u in range(2):
                 nc.sync.dma_start(raw[:, 2 * u : 2 * u + 2, :], rows[a][:, 2 * u : 2 * u + 2, :])
                 if (a, u) == (1, 0):
@@ -45,7 +45,7 @@ def tile_moe_two_lin_relu_kernel(tc, xT, w_words, w_scales, b, gate, offs, dst, 
             raws.append(raw)
         bias = keep.tile([P, E], F32, name="bias")
         weights = {}
-        gates = keep.tile([P, T], F32, name="gates")
+        gates = keep.tile([P, T], F32, name="gates", align_bytes=256)
         scales_in = w_scales.rearrange("e a q n -> q (e a) n").bitcast(I32)
         words_in = w_words.rearrange("e a p n r -> p (e a) (n r)").bitcast(I32)
 
@@ -57,7 +57,7 @@ def tile_moe_two_lin_relu_kernel(tc, xT, w_words, w_scales, b, gate, offs, dst, 
                 )
 
         def load_weights(e0, e1):
-            tile = keep.tile([P, (e1 - e0) * PASSES, N], U32, name=f"weights{e0}", align_bytes=64)
+            tile = keep.tile([P, (e1 - e0) * PASSES, N], U32, name=f"weights{e0}", align_bytes=256)
             nc.sync.dma_start(tile[:].bitcast(I32), words_in[:, e0 * PASSES : e1 * PASSES, :])
             for e in range(e0, e1):
                 for a in range(PASSES):
@@ -71,17 +71,17 @@ def tile_moe_two_lin_relu_kernel(tc, xT, w_words, w_scales, b, gate, offs, dst, 
         nc.sync.dma_start(gates[:], gate)
         load_weights(2, 4)
 
-        words = [keep.tile([P, T], U32, name=f"words{a}", align_bytes=64) for a in range(PASSES)]
-        slot_scales = keep.tile([P, E * C], U8, name="slot_scales", align_bytes=64)
+        words = [keep.tile([P, T], U32, name=f"words{a}", align_bytes=256) for a in range(PASSES)]
+        slot_scales = keep.tile([P, E * C], U8, name="slot_scales", align_bytes=256)
         banks = [psum.tile([N, C], F32, name=f"bank{e}") for e in range(E)]
-        results = [keep.tile([N, 2 * C], F32, name=f"result{h}") for h in range(2)]
-        placed = keep.tile([N, T], F32, name="placed")
-        grouped = [keep.tile([P, T, PACK], BF16, name=f"grouped{a}", align_bytes=64) for a in range(PASSES)]
+        results = [keep.tile([N, 2 * C], F32, name=f"result{h}", align_bytes=256) for h in range(2)]
+        placed = keep.tile([N, T], F32, name="placed", align_bytes=256)
+        grouped = [keep.tile([P, T, PACK], BF16, name=f"grouped{a}", align_bytes=256) for a in range(PASSES)]
         slot_words = {}
 
         def gather_words(a, e0, e1, tag=None):
             name = f"slot_words{a}_{e0}"
-            tile = keep.tile([P, (e1 - e0) * C], U32, name=name, tag=tag or name, align_bytes=64)
+            tile = keep.tile([P, (e1 - e0) * C], U32, name=name, tag=tag or name, align_bytes=256)
             nc.vector.tensor_copy(tile[:], words[a][:].indirect(offsets[:, e0 * C // 16 : e1 * C // 16]))
             for e in range(e0, e1):
                 slot_words[a, e] = tile[:, (e - e0) * C : (e - e0 + 1) * C]

@@ -9,9 +9,9 @@ U8 = mybir.dt.uint8
 FP8X4 = mybir.dt.float8_e4m3fn_x4
 RELU = mybir.ActivationFunctionType.Relu
 MULT = mybir.AluOpType.mult
+ADD = mybir.AluOpType.add
 
 P = 128
-PACK = 4
 K = 1024
 T = 512
 E = 4
@@ -20,9 +20,6 @@ N = 128
 PASSES = 2
 FLOPS = 2 * K * N * T
 
-HALF = T // 2
-PLANE = (4, 0)
-
 
 def tile_moe_two_lin_relu_kernel(tc, xT, w_words, w_scales, b, gate, offs, dst, out):
     nc = tc.nc
@@ -30,18 +27,15 @@ def tile_moe_two_lin_relu_kernel(tc, xT, w_words, w_scales, b, gate, offs, dst, 
         offsets = keep.tile([P, T // 16], U16, name="offsets")
         places = keep.tile([P, T // 16], U16, name="places")
         weight_scales = keep.tile([P, E * PASSES, N], U8, name="weight_scales", align_bytes=256)
-        token_scales = keep.tile([P, T], U8, name="token_scales", align_bytes=256)
         nc.vector.memset(weight_scales[:].rearrange("p g n -> p (g n)").bitcast(I32), 0)
-        nc.vector.memset(token_scales[:].bitcast(I32), 0)
 
-        rows = xT.rearrange("(a p j) t -> a p j t", a=PASSES, j=PACK)
+        rows = xT.rearrange("(a p v j) t -> a v p j t", a=PASSES, v=2, j=2)
         raws = []
-        for a in range(PASSES):
-            raw = keep.tile([P, PACK, T], F32, name=f"raw{a}", tag=f"raw{a}", align_bytes=256)
-            for u in range(2):
-                nc.sync.dma_start(raw[:, 2 * u : 2 * u + 2, :], rows[a][:, 2 * u : 2 * u + 2, :])
-                if (a, u) == (1, 0):
-                    nc.sync.dma_start(offsets[:], offs)
+        for u in range(4):
+            raw = keep.tile([P, 2, T], F32, name=f"raw{u}", tag=f"raw{u}", align_bytes=256)
+            nc.sync.dma_start(raw[:], rows[u // 2][u % 2])
+            if u == 0:
+                nc.sync.dma_start(offsets[:], offs)
             raws.append(raw)
         bias = keep.tile([P, E], F32, name="bias")
         weights = {}
@@ -71,96 +65,121 @@ def tile_moe_two_lin_relu_kernel(tc, xT, w_words, w_scales, b, gate, offs, dst, 
         nc.sync.dma_start(gates[:], gate)
         load_weights(2, 4)
 
-        words = [keep.tile([P, T], U32, name=f"words{a}", align_bytes=256) for a in range(PASSES)]
-        slot_scales = keep.tile([P, E * C], U8, name="slot_scales", align_bytes=256)
+        pairs = [keep.tile([P, T], U32, name=f"pairs{u}", align_bytes=256) for u in range(4)]
+        picked = {}
         banks = [psum.tile([N, C], F32, name=f"bank{e}") for e in range(E)]
-        results = [keep.tile([N, 2 * C], F32, name=f"result{h}", align_bytes=256) for h in range(2)]
-        placed = keep.tile([N, T], F32, name="placed", align_bytes=256)
-        grouped = [keep.tile([P, T, PACK], BF16, name=f"grouped{a}", align_bytes=256) for a in range(PASSES)]
-        slot_words = {}
+        results = keep.tile([N, T], F32, name="results", align_bytes=256)
+        placed = keep.tile([N, 2 * 3 * C], F32, name="placed", align_bytes=256)
+        grouped = {}
+        codes = {}
+        scales = {}
 
-        def gather_words(a, e0, e1, tag=None):
-            name = f"slot_words{a}_{e0}"
-            tile = keep.tile([P, (e1 - e0) * C], U32, name=name, tag=tag or name, align_bytes=256)
-            nc.vector.tensor_copy(tile[:], words[a][:].indirect(offsets[:, e0 * C // 16 : e1 * C // 16]))
+        def by_vector(o, i):
+            nc.vector.tensor_copy(o, i)
+
+        def by_scalar(o, i):
+            nc.scalar.copy(o, i)
+
+        def by_gpsimd(o, i):
+            nc.gpsimd.tensor_scalar(o, i, 1.0, 0.0, MULT, ADD)
+
+        def round_pair(copy, u, t0, t1):
+            copy(
+                pairs[u][:, t0:t1].bitcast(BF16).rearrange("p (t j) -> p t j", j=2),
+                raws[u][:, :, t0:t1].rearrange("p j t -> p t j"),
+            )
+
+        def gather(u, e0, e1, tag=None):
+            window = pairs[u][:].indirect(offsets[:, e0 * C // 16 : e1 * C // 16])
+            if u % 2 == 0:
+                name = f"picked{u // 2}_{e0}"
+                picked[u // 2, e0] = keep.tile([P, 2, (e1 - e0) * C], U32, name=name, tag=tag or name, align_bytes=256)
+            nc.vector.tensor_copy(picked[u // 2, e0][:, u % 2, :], window)
+
+        def gather_in_place(u, e0, e1, tag=None):
+            if u % 2 == 0:
+                name = f"grouped{u // 2}_{e0}"
+                grouped[u // 2, e0] = keep.tile([P, (e1 - e0) * C, 2], U32, name=name, tag=tag or name, align_bytes=256)
+            window = pairs[u][:].indirect(offsets[:, e0 * C // 16 : e1 * C // 16])
+            nc.vector.tensor_copy(grouped[u // 2, e0][:, :, u % 2], window)
+
+        def merge(engine, a, e0, e1, tag=None):
+            name = f"grouped{a}_{e0}"
+            tile = keep.tile([P, (e1 - e0) * C, 2], U32, name=name, tag=tag or name, align_bytes=256)
+            source = picked[a, e0][:].rearrange("p v s -> p s v")
+            if engine == "vector":
+                nc.vector.tensor_copy(tile[:].bitcast(I32), source.bitcast(I32))
+            else:
+                nc.scalar.copy(tile[:], source)
+            grouped[a, e0] = tile
+
+        def quantise(a, e0, e1):
+            width = (e1 - e0) * C
+            code = keep.tile([P, width], U32, name=f"codes{a}_{e0}", align_bytes=256)
+            scale = keep.tile([P, width], U8, name=f"scales{a}_{e0}", align_bytes=256)
+            nc.vector.quantize_mx(
+                out=code[:].bitcast(FP8X4),
+                scales=scale[:],
+                in_=grouped[a, e0][:].rearrange("p s v -> p (s v)").bitcast(BF16),
+            )
             for e in range(e0, e1):
-                slot_words[a, e] = tile[:, (e - e0) * C : (e - e0 + 1) * C]
-
-        def gather_scales(e0, e1):
-            window = token_scales[:].indirect(offsets[:, e0 * C // 16 : e1 * C // 16])
-            nc.vector.tensor_copy(slot_scales[:, e0 * C : e1 * C], window)
+                codes[a, e] = code[:, (e - e0) * C : (e - e0 + 1) * C]
+                scales[a, e] = scale[:, (e - e0) * C : (e - e0 + 1) * C]
 
         def multiply(e, a):
             nc.tensor.matmul_mx(
                 out=banks[e][:],
                 lhsT=weights[e, a].bitcast(FP8X4),
                 lhsT_scale=weight_scales[:, e * PASSES + a, :],
-                rhs=slot_words[a, e].bitcast(FP8X4),
-                rhs_scale=slot_scales[PLANE[a] :, e * C : (e + 1) * C],
+                rhs=codes[a, e].bitcast(FP8X4),
+                rhs_scale=scales[a, e],
                 start=(a == 0),
                 stop=(a == PASSES - 1),
             )
 
         def finish(e):
             multiply(e, 1)
-            nc.scalar.activation(results[e // 2][:, (e % 2) * C : (e % 2 + 1) * C], banks[e][:], RELU, bias=bias[:, e : e + 1])
+            nc.scalar.activation(results[:, e * C : (e + 1) * C], banks[e][:], RELU, bias=bias[:, e : e + 1])
 
-        def scatter(h):
-            j0, j1 = 2 * h * C, 2 * (h + 1) * C
-            nc.vector.tensor_tensor(placed[:].indirect(places[:, j0 // 16 : j1 // 16]), results[h][:], gates[:, j0:j1], MULT)
+        def scatter(e0, e1):
+            j0, j1 = e0 * C, e1 * C
+            nc.vector.tensor_tensor(placed[:].indirect(places[:, j0 // 16 : j1 // 16]), results[:, j0:j1], gates[:, j0:j1], MULT)
 
-        def place_pair(copy, a, u, c0, c1):
-            copy(
-                grouped[a][:, c0:c1, 2 * u : 2 * u + 2],
-                raws[a][:, 2 * u : 2 * u + 2, c0:c1].rearrange("p j t -> p t j"),
-            )
-
-        def place_all(copy, a, c0, c1):
-            copy(
-                grouped[a][:, c0:c1, :].rearrange("p (c i) j -> p c j i", i=2),
-                raws[a][:, :, c0:c1].rearrange("p j (c i) -> p c j i", i=2),
-            )
-
-        def quantise(a, t0, t1):
-            nc.vector.quantize_mx(
-                out=words[a][:, t0:t1].bitcast(FP8X4),
-                scales=token_scales[PLANE[a] :, t0:t1],
-                in_=grouped[a][:, t0:t1, :].rearrange("p t j -> p (t j)"),
-            )
-
-        vector, scalar = nc.vector.tensor_copy, nc.scalar.copy
-
-        def share_second_pair(a):
-            for g0, split in ((0, 176), (HALF, 160)):
-                place_pair(vector, a, 1, g0, g0 + split)
-                place_pair(scalar, a, 1, g0 + split, g0 + HALF)
-
-        place_pair(vector, 0, 0, 0, 352)
-        place_pair(scalar, 0, 0, 352, T)
-        share_second_pair(0)
-        quantise(0, 0, HALF)
-        quantise(0, HALF, T)
-        place_pair(vector, 1, 0, 368, T)
-        gather_words(0, 0, 3)
-        place_pair(scalar, 1, 0, 0, HALF)
-        place_pair(scalar, 1, 0, HALF, 368)
-        share_second_pair(1)
-        quantise(1, 0, HALF)
-        quantise(1, HALF, T)
-        gather_words(0, 3, 4, tag="raw1")
-        gather_scales(0, 2)
-        gather_words(1, 0, 1)
+        round_pair(by_vector, 0, 0, 352)
+        round_pair(by_scalar, 0, 352, T)
+        gather(0, 0, 2)
+        gather(0, 2, 4)
+        round_pair(by_scalar, 1, 0, 288)
+        round_pair(by_gpsimd, 1, 288, T)
+        gather(1, 0, 2)
+        gather(1, 2, 4)
+        round_pair(by_scalar, 2, 0, 288)
+        round_pair(by_gpsimd, 2, 288, T)
+        merge("scalar", 0, 0, 2)
+        gather(2, 0, 1)
+        gather(2, 1, 3)
+        quantise(0, 0, 2)
         multiply(0, 0)
-        finish(0)
         multiply(1, 0)
-        gather_words(1, 1, 2)
+        round_pair(by_scalar, 3, 0, 288)
+        round_pair(by_gpsimd, 3, 288, T)
+        merge("scalar", 0, 2, 4, tag="raw3")
+        gather(3, 0, 1)
+        gather(3, 1, 3)
+        merge("scalar", 1, 0, 1)
+        quantise(0, 2, 4)
+        quantise(1, 0, 1)
+        finish(0)
+        merge("scalar", 1, 1, 3)
+        gather_in_place(2, 3, 4, tag="picked1_0")
+        gather_in_place(3, 3, 4)
+        quantise(1, 1, 3)
         finish(1)
-        gather_scales(2, 4)
-        gather_words(1, 2, 4)
         multiply(2, 0)
-        multiply(3, 0)
         finish(2)
+        quantise(1, 3, 4)
+        multiply(3, 0)
         finish(3)
-        scatter(0)
-        scatter(1)
-        nc.sync.dma_start(out, placed[:])
+        scatter(0, 1)
+        scatter(1, 4)
+        nc.sync.dma_start(out, placed[:, :T])

@@ -37,7 +37,7 @@ def tile_moe_two_lin_relu_kernel(tc, xT, w_words, w_scales, b, gate, offs, dst, 
             if u == 0:
                 nc.sync.dma_start(offsets[:], offs)
             raws.append(raw)
-        bias = keep.tile([P, E], F32, name="bias")
+        bias = keep.tile([P, E - 1], F32, name="bias")
         weights = {}
         gates = keep.tile([P, T], F32, name="gates", align_bytes=256)
         scales_in = w_scales.rearrange("e a q n -> q (e a) n").bitcast(I32)
@@ -57,19 +57,22 @@ def tile_moe_two_lin_relu_kernel(tc, xT, w_words, w_scales, b, gate, offs, dst, 
                 for a in range(PASSES):
                     weights[e, a] = tile[:, (e - e0) * PASSES + a, :]
 
-        nc.sync.dma_start(bias[:], b)
-        load_scales()
-        load_weights(0, 1)
-        load_weights(1, 2)
         nc.sync.dma_start(places[:], dst)
         nc.sync.dma_start(gates[:], gate)
-        load_weights(2, 4)
+        first_bias = keep.tile([P, 1], F32, name="first_bias", align_bytes=256)
+        with nc.allow_non_contiguous_dma(reason="one bias value a partition"):
+            nc.sync.dma_start(first_bias[:], b[:, 0:1])
+        load_scales()
+        load_weights(0, 1)
+        nc.sync.dma_start(bias[:], b[:, 1:])
+        load_weights(1, 4)
+        biases = [first_bias[:]] + [bias[:, e : e + 1] for e in range(E - 1)]
 
         pairs = [keep.tile([P, T], U32, name=f"pairs{u}", align_bytes=256) for u in range(4)]
         picked = {}
         banks = [psum.tile([N, C], F32, name=f"bank{e}") for e in range(E)]
         results = keep.tile([N, T], F32, name="results", align_bytes=256)
-        placed = keep.tile([N, 2 * 3 * C], F32, name="placed", align_bytes=256)
+        placed = keep.tile([N, T], F32, name="placed", align_bytes=256)
         grouped = {}
         codes = {}
         scales = {}
@@ -85,8 +88,8 @@ def tile_moe_two_lin_relu_kernel(tc, xT, w_words, w_scales, b, gate, offs, dst, 
 
         def round_pair(copy, u, t0, t1):
             copy(
-                pairs[u][:, t0:t1].bitcast(BF16).rearrange("p (t j) -> p t j", j=2),
-                raws[u][:, :, t0:t1].rearrange("p j t -> p t j"),
+                pairs[u][:, t0:t1].bitcast(BF16).rearrange("p (c i j) -> p c j i", i=4, j=2),
+                raws[u][:, :, t0:t1].rearrange("p j (c i) -> p c j i", i=4),
             )
 
         def gather(u, e0, e1, tag=None):
@@ -103,14 +106,11 @@ def tile_moe_two_lin_relu_kernel(tc, xT, w_words, w_scales, b, gate, offs, dst, 
             window = pairs[u][:].indirect(offsets[:, e0 * C // 16 : e1 * C // 16])
             nc.vector.tensor_copy(grouped[u // 2, e0][:, :, u % 2], window)
 
-        def merge(engine, a, e0, e1, tag=None):
+        def merge(a, e0, e1, first, tag=None):
             name = f"grouped{a}_{e0}"
             tile = keep.tile([P, (e1 - e0) * C, 2], U32, name=name, tag=tag or name, align_bytes=256)
-            source = picked[a, e0][:].rearrange("p v s -> p s v")
-            if engine == "vector":
-                nc.vector.tensor_copy(tile[:].bitcast(I32), source.bitcast(I32))
-            else:
-                nc.scalar.copy(tile[:], source)
+            source = picked[a, first][:, :, (e0 - first) * C : (e1 - first) * C]
+            nc.scalar.copy(tile[:].rearrange("p (c i) v -> p c v i", i=2), source.rearrange("p v (c i) -> p c v i", i=2))
             grouped[a, e0] = tile
 
         def quantise(a, e0, e1):
@@ -139,7 +139,7 @@ def tile_moe_two_lin_relu_kernel(tc, xT, w_words, w_scales, b, gate, offs, dst, 
 
         def finish(e):
             multiply(e, 1)
-            nc.scalar.activation(results[:, e * C : (e + 1) * C], banks[e][:], RELU, bias=bias[:, e : e + 1])
+            nc.scalar.activation(results[:, e * C : (e + 1) * C], banks[e][:], RELU, bias=biases[e])
 
         def scatter(e0, e1):
             j0, j1 = e0 * C, e1 * C
@@ -149,37 +149,40 @@ def tile_moe_two_lin_relu_kernel(tc, xT, w_words, w_scales, b, gate, offs, dst, 
         round_pair(by_scalar, 0, 352, T)
         gather(0, 0, 2)
         gather(0, 2, 4)
-        round_pair(by_scalar, 1, 0, 288)
-        round_pair(by_gpsimd, 1, 288, T)
+        round_pair(by_scalar, 1, 0, 304)
+        round_pair(by_gpsimd, 1, 304, T)
         gather(1, 0, 2)
         gather(1, 2, 4)
-        round_pair(by_scalar, 2, 0, 288)
-        round_pair(by_gpsimd, 2, 288, T)
-        merge("scalar", 0, 0, 2)
-        gather(2, 0, 1)
+        round_pair(by_scalar, 2, 0, 304)
+        round_pair(by_gpsimd, 2, 304, T)
+        merge(0, 0, 2, 0)
+        gather_in_place(2, 0, 1)
         gather(2, 1, 3)
         quantise(0, 0, 2)
         multiply(0, 0)
         multiply(1, 0)
-        round_pair(by_scalar, 3, 0, 288)
-        round_pair(by_gpsimd, 3, 288, T)
-        merge("scalar", 0, 2, 4, tag="raw3")
-        gather(3, 0, 1)
+        round_pair(by_scalar, 3, 0, 304)
+        round_pair(by_gpsimd, 3, 304, T)
+        merge(0, 2, 4, 2, tag="raw3")
+        gather_in_place(3, 0, 1)
         gather(3, 1, 3)
-        merge("scalar", 1, 0, 1)
-        quantise(0, 2, 4)
         quantise(1, 0, 1)
         finish(0)
-        merge("scalar", 1, 1, 3)
-        gather_in_place(2, 3, 4, tag="picked1_0")
-        gather_in_place(3, 3, 4)
-        quantise(1, 1, 3)
+        quantise(0, 2, 4)
+        gather(2, 3, 4, tag="picked0_2")
+        gather(3, 3, 4)
+        merge(1, 1, 2, 1)
+        merge(1, 2, 3, 1)
+        quantise(1, 1, 2)
         finish(1)
+        quantise(1, 2, 3)
         multiply(2, 0)
         finish(2)
+        merge(1, 3, 4, 3, tag="first_bias")
+        scatter(0, 1)
         quantise(1, 3, 4)
         multiply(3, 0)
         finish(3)
-        scatter(0, 1)
-        scatter(1, 4)
-        nc.sync.dma_start(out, placed[:, :T])
+        scatter(1, 2)
+        scatter(2, 4)
+        nc.sync.dma_start(out, placed[:])

@@ -149,20 +149,20 @@ def tile_moe_two_lin_relu_kernel(tc, xT, w_words, w_scales, b, gate, offs, dst, 
         round_pair(by_scalar, 0, 352, T)
         gather(0, 0, 2)
         gather(0, 2, 4)
-        round_pair(by_scalar, 1, 0, 304)
-        round_pair(by_gpsimd, 1, 304, T)
+        round_pair(by_scalar, 1, 0, 272)
+        round_pair(by_gpsimd, 1, 272, T)
         gather(1, 0, 2)
         gather(1, 2, 4)
-        round_pair(by_scalar, 2, 0, 304)
-        round_pair(by_gpsimd, 2, 304, T)
+        round_pair(by_scalar, 2, 0, 272)
+        round_pair(by_gpsimd, 2, 272, T)
         merge(0, 0, 2, 0)
         gather_in_place(2, 0, 1)
         gather(2, 1, 3)
         quantise(0, 0, 2)
         multiply(0, 0)
         multiply(1, 0)
-        round_pair(by_scalar, 3, 0, 304)
-        round_pair(by_gpsimd, 3, 304, T)
+        round_pair(by_scalar, 3, 0, 288)
+        round_pair(by_gpsimd, 3, 288, T)
         merge(0, 2, 4, 2, tag="raw3")
         gather_in_place(3, 0, 1)
         gather(3, 1, 3)

@@ -8,8 +8,10 @@ U16 = mybir.dt.uint16
 U8 = mybir.dt.uint8
 FP8X4 = mybir.dt.float8_e4m3fn_x4
 RELU = mybir.ActivationFunctionType.Relu
+COPY = mybir.ActivationFunctionType.Copy
 MULT = mybir.AluOpType.mult
 ADD = mybir.AluOpType.add
+MAX = mybir.AluOpType.max
 
 P = 128
 K = 1024
@@ -18,6 +20,7 @@ E = 4
 C = 128
 N = 128
 PASSES = 2
+SCALAR_SLOTS = 320
 FLOPS = 2 * K * N * T
 
 
@@ -27,7 +30,11 @@ def tile_moe_two_lin_relu_kernel(tc, xT, w_words, w_scales, b, gate, offs, dst, 
         offsets = keep.tile([P, T // 16], U16, name="offsets")
         places = keep.tile([P, T // 16], U16, name="places")
         weight_scales = keep.tile([P, E * PASSES, N], U8, name="weight_scales", align_bytes=256)
+        placed_v = keep.tile([N, T], F32, name="placed_v", align_bytes=256)
+        placed_s = keep.tile([N, T], F32, name="placed_s", align_bytes=256)
         nc.vector.memset(weight_scales[:].rearrange("p g n -> p (g n)").bitcast(I32), 0)
+        nc.vector.memset(placed_v[:], 0.0)
+        nc.vector.memset(placed_s[:], 0.0)
 
         rows = xT.rearrange("(a p v j) t -> a v p j t", a=PASSES, v=2, j=2)
         raws = []
@@ -37,7 +44,7 @@ def tile_moe_two_lin_relu_kernel(tc, xT, w_words, w_scales, b, gate, offs, dst, 
             if u == 0:
                 nc.sync.dma_start(offsets[:], offs)
             raws.append(raw)
-        bias = keep.tile([P, E - 1], F32, name="bias")
+        bias = keep.tile([P, E], F32, name="bias")
         weights = {}
         gates = keep.tile([P, T], F32, name="gates", align_bytes=256)
         scales_in = w_scales.rearrange("e a q n -> q (e a) n").bitcast(I32)
@@ -59,20 +66,16 @@ def tile_moe_two_lin_relu_kernel(tc, xT, w_words, w_scales, b, gate, offs, dst, 
 
         nc.sync.dma_start(places[:], dst)
         nc.sync.dma_start(gates[:], gate)
-        first_bias = keep.tile([P, 1], F32, name="first_bias", align_bytes=256)
-        with nc.allow_non_contiguous_dma(reason="one bias value a partition"):
-            nc.sync.dma_start(first_bias[:], b[:, 0:1])
+        nc.sync.dma_start(bias[:], b)
         load_scales()
         load_weights(0, 1)
-        nc.sync.dma_start(bias[:], b[:, 1:])
         load_weights(1, 4)
-        biases = [first_bias[:]] + [bias[:, e : e + 1] for e in range(E - 1)]
 
         pairs = [keep.tile([P, T], U32, name=f"pairs{u}", align_bytes=256) for u in range(4)]
         picked = {}
         banks = [psum.tile([N, C], F32, name=f"bank{e}") for e in range(E)]
         results = keep.tile([N, T], F32, name="results", align_bytes=256)
-        placed = keep.tile([N, T], F32, name="placed", align_bytes=256)
+        gated = keep.tile([N, SCALAR_SLOTS], F32, name="gated", align_bytes=256)
         grouped = {}
         codes = {}
         scales = {}
@@ -115,7 +118,7 @@ def tile_moe_two_lin_relu_kernel(tc, xT, w_words, w_scales, b, gate, offs, dst, 
 
         def quantise(a, e0, e1):
             width = (e1 - e0) * C
-            code = keep.tile([P, width], U32, name=f"codes{a}_{e0}", align_bytes=256)
+            code = keep.tile([P, width], U32, name=f"codes{a}_{e0}", tag=f"codes{a}_{e0}", align_bytes=256)
             scale = keep.tile([P, width], U8, name=f"scales{a}_{e0}", align_bytes=256)
             nc.vector.quantize_mx(
                 out=code[:].bitcast(FP8X4),
@@ -137,13 +140,20 @@ def tile_moe_two_lin_relu_kernel(tc, xT, w_words, w_scales, b, gate, offs, dst, 
                 stop=(a == PASSES - 1),
             )
 
-        def finish(e):
-            multiply(e, 1)
-            nc.scalar.activation(results[:, e * C : (e + 1) * C], banks[e][:], RELU, bias=biases[e])
+        def activate_by_scalar(e):
+            nc.scalar.activation(results[:, e * C : (e + 1) * C], banks[e][:], RELU, bias=bias[:, e : e + 1])
 
-        def scatter(e0, e1):
-            j0, j1 = e0 * C, e1 * C
-            nc.vector.tensor_tensor(placed[:].indirect(places[:, j0 // 16 : j1 // 16]), results[:, j0:j1], gates[:, j0:j1], MULT)
+        def activate_by_vector(e):
+            nc.vector.tensor_scalar(results[:, e * C : (e + 1) * C], banks[e][:], bias[:, e : e + 1], 0.0, ADD, MAX)
+
+        def weigh(j0, j1):
+            nc.vector.tensor_tensor(gated[:, j0:j1], results[:, j0:j1], gates[:, j0:j1], MULT)
+
+        def scatter_by_scalar(j0, j1):
+            nc.scalar.activation(placed_s[:].indirect(places[:, j0 // 16 : j1 // 16]), gated[:, j0:j1], COPY)
+
+        def scatter_by_vector(j0, j1):
+            nc.vector.tensor_tensor(placed_v[:].indirect(places[:, j0 // 16 : j1 // 16]), results[:, j0:j1], gates[:, j0:j1], MULT)
 
         round_pair(by_vector, 0, 0, 352)
         round_pair(by_scalar, 0, 352, T)
@@ -167,22 +177,32 @@ def tile_moe_two_lin_relu_kernel(tc, xT, w_words, w_scales, b, gate, offs, dst, 
         gather_in_place(3, 0, 1)
         gather(3, 1, 3)
         quantise(1, 0, 1)
-        finish(0)
-        quantise(0, 2, 4)
+        multiply(0, 1)
         gather(2, 3, 4, tag="picked0_2")
         gather(3, 3, 4)
         merge(1, 1, 2, 1)
         merge(1, 2, 3, 1)
+        activate_by_scalar(0)
+        merge(1, 3, 4, 3, tag="codes1_0")
         quantise(1, 1, 2)
-        finish(1)
+        multiply(1, 1)
+        quantise(0, 2, 4)
         quantise(1, 2, 3)
         multiply(2, 0)
-        finish(2)
-        merge(1, 3, 4, 3, tag="first_bias")
-        scatter(0, 1)
+        multiply(2, 1)
+        weigh(0, C)
         quantise(1, 3, 4)
         multiply(3, 0)
-        finish(3)
-        scatter(1, 2)
-        scatter(2, 4)
-        nc.sync.dma_start(out, placed[:])
+        multiply(3, 1)
+        scatter_by_scalar(0, C)
+        activate_by_vector(1)
+        activate_by_vector(2)
+        activate_by_vector(3)
+        weigh(C, SCALAR_SLOTS)
+        scatter_by_scalar(C, SCALAR_SLOTS)
+        scatter_by_vector(SCALAR_SLOTS, T)
+        joined = keep.tile([N, T], F32, name="joined", align_bytes=256)
+        for h in range(2):
+            half = slice(h * T // 2, (h + 1) * T // 2)
+            nc.vector.tensor_tensor(joined[:, half], placed_v[:, half], placed_s[:, half], ADD)
+            nc.sync.dma_start(out[:, half], joined[:, half])

@@ -197,7 +197,7 @@ def tile_moe_two_lin_relu_kernel(tc, xT, w_words, w_scales, b, gate, offs, dst, 
         scatter_by_scalar(0, C)
         activate_by_vector(1)
         activate_by_vector(2)
-        activate_by_vector(3)
+        activate_by_scalar(3)
         weigh(C, SCALAR_SLOTS)
         scatter_by_scalar(C, SCALAR_SLOTS)
         scatter_by_vector(SCALAR_SLOTS, T)

@@ -68,15 +68,17 @@ def tile_moe_two_lin_relu_kernel(tc, xT, w_words, w_scales, b, gate, offs, dst, 
         nc.sync.dma_start(gates[:], gate)
         nc.sync.dma_start(bias[:], b)
         load_scales()
-        load_weights(0, 1)
-        load_weights(1, 4)
+        load_weights(0, 2)
+        load_weights(2, 4)
 
-        pairs = [keep.tile([P, T], U32, name=f"pairs{u}", align_bytes=256) for u in range(4)]
-        picked = {}
+        opening = keep.tile([P, 2 * T], U32, name="opening", align_bytes=256)
+        pairs = [opening[:, T:], opening[:, :T]] + [keep.tile([P, T], U32, name=f"pairs{u}", align_bytes=256)[:] for u in (2, 3)]
+        picked = keep.tile([P, 2, T], U32, name="picked", tag="picked", align_bytes=256)
+        middle = keep.tile([P, 2, 2 * C], U32, name="middle", align_bytes=256)
         banks = [psum.tile([N, C], F32, name=f"bank{e}") for e in range(E)]
-        results = keep.tile([N, T], F32, name="results", align_bytes=256)
+        early = keep.tile([N, C], F32, name="early", align_bytes=256)
+        results = {0: early[:]}
         gated = keep.tile([N, SCALAR_SLOTS], F32, name="gated", align_bytes=256)
-        grouped = {}
         codes = {}
         scales = {}
 
@@ -95,39 +97,27 @@ def tile_moe_two_lin_relu_kernel(tc, xT, w_words, w_scales, b, gate, offs, dst, 
                 raws[u][:, :, t0:t1].rearrange("p j (c i) -> p c j i", i=4),
             )
 
-        def gather(u, e0, e1, tag=None):
-            window = pairs[u][:].indirect(offsets[:, e0 * C // 16 : e1 * C // 16])
-            if u % 2 == 0:
-                name = f"picked{u // 2}_{e0}"
-                picked[u // 2, e0] = keep.tile([P, 2, (e1 - e0) * C], U32, name=name, tag=tag or name, align_bytes=256)
-            nc.vector.tensor_copy(picked[u // 2, e0][:, u % 2, :], window)
+        def gather(into, window, e0, e1):
+            nc.vector.tensor_copy(into, window.indirect(offsets[:, e0 * C // 16 : e1 * C // 16]))
 
-        def gather_in_place(u, e0, e1, tag=None):
-            if u % 2 == 0:
-                name = f"grouped{u // 2}_{e0}"
-                grouped[u // 2, e0] = keep.tile([P, (e1 - e0) * C, 2], U32, name=name, tag=tag or name, align_bytes=256)
-            window = pairs[u][:].indirect(offsets[:, e0 * C // 16 : e1 * C // 16])
-            nc.vector.tensor_copy(grouped[u // 2, e0][:, :, u % 2], window)
+        def group(name, blocks, tag=None):
+            return keep.tile([P, blocks * C, 2], U32, name=name, tag=tag or name, align_bytes=256)
 
-        def merge(a, e0, e1, first, tag=None):
-            name = f"grouped{a}_{e0}"
-            tile = keep.tile([P, (e1 - e0) * C, 2], U32, name=name, tag=tag or name, align_bytes=256)
-            source = picked[a, first][:, :, (e0 - first) * C : (e1 - first) * C]
-            nc.scalar.copy(tile[:].rearrange("p (c i) v -> p c v i", i=2), source.rearrange("p v (c i) -> p c v i", i=2))
-            grouped[a, e0] = tile
+        def merge(into, source):
+            nc.scalar.copy(into.rearrange("p (c i) v -> p c v i", i=2), source.rearrange("p v (c i) -> p c v i", i=2))
 
-        def quantise(a, e0, e1):
-            width = (e1 - e0) * C
-            code = keep.tile([P, width], U32, name=f"codes{a}_{e0}", tag=f"codes{a}_{e0}", align_bytes=256)
-            scale = keep.tile([P, width], U8, name=f"scales{a}_{e0}", align_bytes=256)
+        def quantise(name, grouped, parts):
+            width = len(parts) * C
+            code = keep.tile([P, width], U32, name=f"codes_{name}", tag=f"codes_{name}", align_bytes=256)
+            scale = keep.tile([P, width], U8, name=f"scales_{name}", align_bytes=256)
             nc.vector.quantize_mx(
                 out=code[:].bitcast(FP8X4),
                 scales=scale[:],
-                in_=grouped[a, e0][:].rearrange("p s v -> p (s v)").bitcast(BF16),
+                in_=grouped[:].rearrange("p s v -> p (s v)").bitcast(BF16),
             )
-            for e in range(e0, e1):
-                codes[a, e] = code[:, (e - e0) * C : (e - e0 + 1) * C]
-                scales[a, e] = scale[:, (e - e0) * C : (e - e0 + 1) * C]
+            for g, part in enumerate(parts):
+                codes[part] = code[:, g * C : (g + 1) * C]
+                scales[part] = scale[:, g * C : (g + 1) * C]
 
         def multiply(e, a):
             nc.tensor.matmul_mx(
@@ -141,66 +131,70 @@ def tile_moe_two_lin_relu_kernel(tc, xT, w_words, w_scales, b, gate, offs, dst, 
             )
 
         def activate_by_scalar(e):
-            nc.scalar.activation(results[:, e * C : (e + 1) * C], banks[e][:], RELU, bias=bias[:, e : e + 1])
+            nc.scalar.activation(results[e], banks[e][:], RELU, bias=bias[:, e : e + 1])
 
         def activate_by_vector(e):
-            nc.vector.tensor_scalar(results[:, e * C : (e + 1) * C], banks[e][:], bias[:, e : e + 1], 0.0, ADD, MAX)
+            nc.vector.tensor_scalar(results[e], banks[e][:], bias[:, e : e + 1], 0.0, ADD, MAX)
 
-        def weigh(j0, j1):
-            nc.vector.tensor_tensor(gated[:, j0:j1], results[:, j0:j1], gates[:, j0:j1], MULT)
+        def weigh(values, j0, j1):
+            nc.vector.tensor_tensor(gated[:, j0:j1], values, gates[:, j0:j1], MULT)
 
         def scatter_by_scalar(j0, j1):
             nc.scalar.activation(placed_s[:].indirect(places[:, j0 // 16 : j1 // 16]), gated[:, j0:j1], COPY)
 
-        def scatter_by_vector(j0, j1):
-            nc.vector.tensor_tensor(placed_v[:].indirect(places[:, j0 // 16 : j1 // 16]), results[:, j0:j1], gates[:, j0:j1], MULT)
+        def scatter_by_vector(values, j0, j1):
+            nc.vector.tensor_tensor(placed_v[:].indirect(places[:, j0 // 16 : j1 // 16]), values, gates[:, j0:j1], MULT)
 
         round_pair(by_vector, 0, 0, 352)
         round_pair(by_scalar, 0, 352, T)
-        gather(0, 0, 2)
-        gather(0, 2, 4)
+        gather(picked[:, 0, : 2 * C], pairs[0], 0, 2)
+        gather(picked[:, 0, 2 * C :], pairs[0], 2, 4)
         round_pair(by_scalar, 1, 0, 272)
         round_pair(by_gpsimd, 1, 272, T)
-        gather(1, 0, 2)
-        gather(1, 2, 4)
+        gather(picked[:, 1, :], opening[:, : T + 2 * C], 0, 4)
         round_pair(by_scalar, 2, 0, 272)
         round_pair(by_gpsimd, 2, 272, T)
-        merge(0, 0, 2, 0)
-        gather_in_place(2, 0, 1)
-        gather(2, 1, 3)
-        quantise(0, 0, 2)
-        multiply(0, 0)
-        multiply(1, 0)
+        first = group("first", 3)
+        gather(first[:, :C, 0], pairs[2], 0, 1)
+        gather(middle[:, 0, :], pairs[2], 1, 3)
         round_pair(by_scalar, 3, 0, 288)
         round_pair(by_gpsimd, 3, 288, T)
-        merge(0, 2, 4, 2, tag="raw3")
-        gather_in_place(3, 0, 1)
-        gather(3, 1, 3)
-        quantise(1, 0, 1)
+        merge(first[:, C:, :], picked[:, :, : 2 * C])
+        second = group("second", 3, tag="raw3")
+        merge(second[:, : 2 * C, :], picked[:, :, 2 * C :])
+        gather(first[:, :C, 1], pairs[3], 0, 1)
+        gather(middle[:, 1, :], pairs[3], 1, 3)
+        quantise("first", first, [(1, 0), (0, 0), (0, 1)])
+        multiply(0, 0)
         multiply(0, 1)
-        gather(2, 3, 4, tag="picked0_2")
-        gather(3, 3, 4)
-        merge(1, 1, 2, 1)
-        merge(1, 2, 3, 1)
+        multiply(1, 0)
+        last = keep.tile([P, 2, C], U32, name="last", tag="picked", align_bytes=256)
+        gather(last[:, 0, :], pairs[2], 3, 4)
+        gather(last[:, 1, :], pairs[3], 3, 4)
+        merge(second[:, 2 * C :, :], middle[:, :, :C])
+        third = group("third", 1)
+        merge(third[:], middle[:, :, C:])
         activate_by_scalar(0)
-        merge(1, 3, 4, 3, tag="codes1_0")
-        quantise(1, 1, 2)
-        multiply(1, 1)
-        quantise(0, 2, 4)
-        quantise(1, 2, 3)
+        fourth = group("fourth", 1, tag="codes_first")
+        merge(fourth[:], last[:])
+        quantise("second", second, [(0, 2), (0, 3), (1, 1)])
         multiply(2, 0)
+        multiply(1, 1)
+        quantise("third", third, [(1, 2)])
         multiply(2, 1)
-        weigh(0, C)
-        quantise(1, 3, 4)
         multiply(3, 0)
+        weigh(early[:], 0, C)
+        quantise("fourth", fourth, [(1, 3)])
         multiply(3, 1)
         scatter_by_scalar(0, C)
+        late = keep.tile([N, T - C], F32, name="late", tag="picked", align_bytes=256)
+        results.update({e: late[:, (e - 1) * C : e * C] for e in range(1, E)})
         activate_by_vector(1)
         activate_by_vector(2)
         activate_by_scalar(3)
-        weigh(C, SCALAR_SLOTS)
+        weigh(late[:, : SCALAR_SLOTS - C], C, SCALAR_SLOTS)
         scatter_by_scalar(C, SCALAR_SLOTS)
-        scatter_by_vector(SCALAR_SLOTS, T)
+        scatter_by_vector(late[:, SCALAR_SLOTS - C :], SCALAR_SLOTS, T)
         joined = keep.tile([N, T], F32, name="joined", align_bytes=256)
         for h in range(2):
             half = slice(h * T // 2, (h + 1) * T // 2)

@@ -64,12 +64,11 @@ def tile_moe_two_lin_relu_kernel(tc, xT, w_words, w_scales, b, gate, offs, dst, 
                 for a in range(PASSES):
                     weights[e, a] = tile[:, (e - e0) * PASSES + a, :]
 
-        nc.sync.dma_start(places[:], dst)
-        nc.sync.dma_start(gates[:], gate)
-        nc.sync.dma_start(bias[:], b)
         load_scales()
-        load_weights(0, 2)
-        load_weights(2, 4)
+        nc.sync.dma_start(bias[:], b)
+        load_weights(0, 4)
+        nc.sync.dma_start(gates[:], gate)
+        nc.sync.dma_start(places[:], dst)
 
         opening = keep.tile([P, 2 * T], U32, name="opening", align_bytes=256)
         pairs = [opening[:, T:], opening[:, :T]] + [keep.tile([P, T], U32, name=f"pairs{u}", align_bytes=256)[:] for u in (2, 3)]
@@ -196,7 +195,6 @@ def tile_moe_two_lin_relu_kernel(tc, xT, w_words, w_scales, b, gate, offs, dst, 
         scatter_by_scalar(C, SCALAR_SLOTS)
         scatter_by_vector(late[:, SCALAR_SLOTS - C :], SCALAR_SLOTS, T)
         joined = keep.tile([N, T], F32, name="joined", align_bytes=256)
-        for h in range(2):
-            half = slice(h * T // 2, (h + 1) * T // 2)
-            nc.vector.tensor_tensor(joined[:, half], placed_v[:, half], placed_s[:, half], ADD)
-            nc.sync.dma_start(out[:, half], joined[:, half])
+        for part in (slice(0, 128), slice(128, 320), slice(320, T)):
+            nc.vector.tensor_tensor(joined[:, part], placed_v[:, part], placed_s[:, part], ADD)
+            nc.sync.dma_start(out[:, part], joined[:, part])

import concourse.mybir as mybir

F32 = mybir.dt.float32
BF16 = mybir.dt.bfloat16
I32 = mybir.dt.int32
U32 = mybir.dt.uint32
U16 = mybir.dt.uint16
U8 = mybir.dt.uint8
FP8X4 = mybir.dt.float8_e4m3fn_x4
RELU = mybir.ActivationFunctionType.Relu
COPY = mybir.ActivationFunctionType.Copy
MULT = mybir.AluOpType.mult
ADD = mybir.AluOpType.add
MAX = mybir.AluOpType.max

P = 128
K = 1024
T = 512
E = 4
C = 128
N = 128
PASSES = 2
SCALAR_SLOTS = 320
FLOPS = 2 * K * N * T


def tile_moe_two_lin_relu_kernel(tc, xT, w_words, w_scales, b, gate, offs, dst, out):
    nc = tc.nc
    with tc.tile_pool(name="keep", bufs=1) as keep, tc.psum_pool(name="psum", bufs=1) as psum:
        offsets = keep.tile([P, T // 16], U16, name="offsets")
        places = keep.tile([P, T // 16], U16, name="places")
        weight_scales = keep.tile([P, E * PASSES, N], U8, name="weight_scales", align_bytes=256)
        placed_v = keep.tile([N, T], F32, name="placed_v", align_bytes=256)
        placed_s = keep.tile([N, T], F32, name="placed_s", align_bytes=256)
        nc.vector.memset(weight_scales[:].rearrange("p g n -> p (g n)").bitcast(I32), 0)
        nc.vector.memset(placed_v[:], 0.0)
        nc.vector.memset(placed_s[:], 0.0)

        rows = xT.rearrange("(a p v j) t -> a v p j t", a=PASSES, v=2, j=2)
        raws = []
        for u in range(4):
            raw = keep.tile([P, 2, T], F32, name=f"raw{u}", tag=f"raw{u}", align_bytes=256)
            nc.sync.dma_start(raw[:], rows[u // 2][u % 2])
            if u == 0:
                nc.sync.dma_start(offsets[:], offs)
            raws.append(raw)
        bias = keep.tile([P, E], F32, name="bias")
        weights = {}
        gates = keep.tile([P, T], F32, name="gates", align_bytes=256)
        scales_in = w_scales.rearrange("e a q n -> q (e a) n").bitcast(I32)
        words_in = w_words.rearrange("e a p n r -> p (e a) (n r)").bitcast(I32)

        def load_scales():
            for q in range(4):
                nc.sync.dma_start(
                    weight_scales[32 * q : 32 * q + 4, :, :].bitcast(I32),
                    scales_in[4 * q : 4 * q + 4, :, :],
                )

        def load_weights(e0, e1):
            tile = keep.tile([P, (e1 - e0) * PASSES, N], U32, name=f"weights{e0}", align_bytes=256)
            nc.sync.dma_start(tile[:].bitcast(I32), words_in[:, e0 * PASSES : e1 * PASSES, :])
            for e in range(e0, e1):
                for a in range(PASSES):
                    weights[e, a] = tile[:, (e - e0) * PASSES + a, :]

        load_scales()
        nc.sync.dma_start(bias[:], b)
        load_weights(0, 4)
        nc.sync.dma_start(gates[:], gate)
        nc.sync.dma_start(places[:], dst)

        opening = keep.tile([P, 2 * T], U32, name="opening", align_bytes=256)
        pairs = [opening[:, T:], opening[:, :T]] + [keep.tile([P, T], U32, name=f"pairs{u}", align_bytes=256)[:] for u in (2, 3)]
        picked = keep.tile([P, 2, T], U32, name="picked", tag="picked", align_bytes=256)
        middle = keep.tile([P, 2, 2 * C], U32, name="middle", align_bytes=256)
        banks = [psum.tile([N, C], F32, name=f"bank{e}") for e in range(E)]
        early = keep.tile([N, C], F32, name="early", align_bytes=256)
        results = {0: early[:]}
        gated = keep.tile([N, SCALAR_SLOTS], F32, name="gated", align_bytes=256)
        codes = {}
        scales = {}

        def by_vector(o, i):
            nc.vector.tensor_copy(o, i)

        def by_scalar(o, i):
            nc.scalar.copy(o, i)

        def by_gpsimd(o, i):
            nc.gpsimd.tensor_scalar(o, i, 1.0, 0.0, MULT, ADD)

        def round_pair(copy, u, t0, t1):
            copy(
                pairs[u][:, t0:t1].bitcast(BF16).rearrange("p (c i j) -> p c j i", i=4, j=2),
                raws[u][:, :, t0:t1].rearrange("p j (c i) -> p c j i", i=4),
            )

        def gather(into, window, e0, e1):
            nc.vector.tensor_copy(into, window.indirect(offsets[:, e0 * C // 16 : e1 * C // 16]))

        def group(name, blocks, tag=None):
            return keep.tile([P, blocks * C, 2], U32, name=name, tag=tag or name, align_bytes=256)

        def merge(into, source):
            nc.scalar.copy(into.rearrange("p (c i) v -> p c v i", i=2), source.rearrange("p v (c i) -> p c v i", i=2))

        def quantise(name, grouped, parts):
            width = len(parts) * C
            code = keep.tile([P, width], U32, name=f"codes_{name}", tag=f"codes_{name}", align_bytes=256)
            scale = keep.tile([P, width], U8, name=f"scales_{name}", align_bytes=256)
            nc.vector.quantize_mx(
                out=code[:].bitcast(FP8X4),
                scales=scale[:],
                in_=grouped[:].rearrange("p s v -> p (s v)").bitcast(BF16),
            )
            for g, part in enumerate(parts):
                codes[part] = code[:, g * C : (g + 1) * C]
                scales[part] = scale[:, g * C : (g + 1) * C]

        def multiply(e, a):
            nc.tensor.matmul_mx(
                out=banks[e][:],
                lhsT=weights[e, a].bitcast(FP8X4),
                lhsT_scale=weight_scales[:, e * PASSES + a, :],
                rhs=codes[a, e].bitcast(FP8X4),
                rhs_scale=scales[a, e],
                start=(a == 0),
                stop=(a == PASSES - 1),
            )

        def activate_by_scalar(e):
            nc.scalar.activation(results[e], banks[e][:], RELU, bias=bias[:, e : e + 1])

        def activate_by_vector(e):
            nc.vector.tensor_scalar(results[e], banks[e][:], bias[:, e : e + 1], 0.0, ADD, MAX)

        def weigh(values, j0, j1):
            nc.vector.tensor_tensor(gated[:, j0:j1], values, gates[:, j0:j1], MULT)

        def scatter_by_scalar(j0, j1):
            nc.scalar.activation(placed_s[:].indirect(places[:, j0 // 16 : j1 // 16]), gated[:, j0:j1], COPY)

        def scatter_by_vector(values, j0, j1):
            nc.vector.tensor_tensor(placed_v[:].indirect(places[:, j0 // 16 : j1 // 16]), values, gates[:, j0:j1], MULT)

        round_pair(by_vector, 0, 0, 352)
        round_pair(by_scalar, 0, 352, T)
        gather(picked[:, 0, : 2 * C], pairs[0], 0, 2)
        gather(picked[:, 0, 2 * C :], pairs[0], 2, 4)
        round_pair(by_scalar, 1, 0, 272)
        round_pair(by_gpsimd, 1, 272, T)
        gather(picked[:, 1, :], opening[:, : T + 2 * C], 0, 4)
        round_pair(by_scalar, 2, 0, 272)
        round_pair(by_gpsimd, 2, 272, T)
        first = group("first", 3)
        gather(first[:, :C, 0], pairs[2], 0, 1)
        gather(middle[:, 0, :], pairs[2], 1, 3)
        round_pair(by_scalar, 3, 0, 288)
        round_pair(by_gpsimd, 3, 288, T)
        merge(first[:, C:, :], picked[:, :, : 2 * C])
        second = group("second", 3, tag="raw3")
        merge(second[:, : 2 * C, :], picked[:, :, 2 * C :])
        gather(first[:, :C, 1], pairs[3], 0, 1)
        gather(middle[:, 1, :], pairs[3], 1, 3)
        quantise("first", first, [(1, 0), (0, 0), (0, 1)])
        multiply(0, 0)
        multiply(0, 1)
        multiply(1, 0)
        last = keep.tile([P, 2, C], U32, name="last", tag="picked", align_bytes=256)
        gather(last[:, 0, :], pairs[2], 3, 4)
        gather(last[:, 1, :], pairs[3], 3, 4)
        merge(second[:, 2 * C :, :], middle[:, :, :C])
        third = group("third", 1)
        merge(third[:], middle[:, :, C:])
        activate_by_scalar(0)
        fourth = group("fourth", 1, tag="codes_first")
        merge(fourth[:], last[:])
        quantise("second", second, [(0, 2), (0, 3), (1, 1)])
        multiply(2, 0)
        multiply(1, 1)
        quantise("third", third, [(1, 2)])
        multiply(2, 1)
        multiply(3, 0)
        weigh(early[:], 0, C)
        quantise("fourth", fourth, [(1, 3)])
        multiply(3, 1)
        scatter_by_scalar(0, C)
        late = keep.tile([N, T - C], F32, name="late", tag="picked", align_bytes=256)
        results.update({e: late[:, (e - 1) * C : e * C] for e in range(1, E)})
        activate_by_vector(1)
        activate_by_vector(2)
        activate_by_scalar(3)
        weigh(late[:, : SCALAR_SLOTS - C], C, SCALAR_SLOTS)
        scatter_by_scalar(C, SCALAR_SLOTS)
        scatter_by_vector(late[:, SCALAR_SLOTS - C :], SCALAR_SLOTS, T)
        joined = keep.tile([N, T], F32, name="joined", align_bytes=256)
        for part in (slice(0, 128), slice(128, 320), slice(320, T)):
            nc.vector.tensor_tensor(joined[:, part], placed_v[:, part], placed_s[:, part], ADD)
            nc.sync.dma_start(out[:, part], joined[:, part])
